import numpy as np, ml_dtypes
CORES = [3,11,19,27,35,43,51,59]
N = 8
import mx_ref
BF = ml_dtypes.bfloat16
def gcols(t, e):
    v = np.concatenate([t.reshape(8, 16, -1, 4), np.zeros((8, 16, 1, 4), BF)], axis=2)
    return np.ascontiguousarray(np.stack([v[g][:, e[g]] for g in range(8)])).reshape(128, -1)
def tile(rs):
    return np.stack(rs, axis=2).reshape(128, -1).astype(BF)
def pick(q, e):
    c = np.concatenate([q[0].reshape(128, -1, 4), np.zeros((128, 1, 4), np.uint8)], axis=1); s = np.concatenate([q[1], np.ones((16, 1), np.uint8)], axis=1)
    return (np.ascontiguousarray(c[:, e].reshape(128, -1)), np.ascontiguousarray(s[:, e]))
def join(*qs):
    return (np.concatenate([q[0] for q in qs], axis=1), np.concatenate([q[1] for q in qs], axis=1))
def put(q, e, v):
    c, s = q[0].reshape(128, -1, 4).copy(), q[1].copy(); c[:, e] = v[0].reshape(128, -1, 4); s[:, e] = v[1]
    return (c.reshape(128, -1), s)
def pk(c, s):
    return (np.ascontiguousarray(c), mx_ref.live(s))
def emit(q):
    return q[0], q[1]
def packed(v, rng):
    q = [mx_ref.quantize(np.ascontiguousarray(v[r])) for r in range(N)]
    return np.stack([a for a, b in q]), np.stack([mx_ref.plane(b, rng) for a, b in q])
def values_of_codes():
    e, c = np.zeros((128, 128, 4), np.float32), np.zeros((128, 2, 4), np.uint8)
    e[np.arange(128), np.arange(128), 0] = 1
    c[:127, :, 0] = np.arange(256).reshape(2, 128).T[:127]
    return mx_ref.matmul(mx_ref.quantize(e.reshape(128, 512).astype(BF)), (c.reshape(128, 8), np.full((16, 2), 127, np.uint8))).T.reshape(-1).astype(np.float64)
CODE_VALUE, SCALE_VALUE = values_of_codes(), 2.0 ** (np.arange(256) - 127.0)
def decode(q):
    return (CODE_VALUE[q[0]].reshape(16, 8, -1, 4) * SCALE_VALUE[q[1]][:, None, :, None] + 0.0).reshape(128, -1).astype(np.float32)
def f(rng, *shape):
    return mx_ref.flush((rng.standard_normal(shape, dtype=np.float32) * np.exp2(rng.integers(-2, 3, shape[:-1] + (1,)))).astype(BF))
def wide(rng, *shape, cols=0):
    v = rng.standard_normal(shape, dtype=np.float32) * np.exp2(rng.integers(-12, 13, shape)).astype(np.float32)
    if cols: v *= np.repeat(np.exp2(rng.integers(-cols, cols + 1, shape[:-2] + (1, shape[-1] // 4))) * (rng.random(shape[:-2] + (1, shape[-1] // 4)) > 0.0625), 4, axis=-1).astype(np.float32)
    return mx_ref.flush(v.astype(BF))
C, M, R = 384, 192, 3
def meet(n):
    i = np.arange(n)
    q = np.stack([i] * 4 + [n - 1 - i] * 4)
    for h in range(1, 8):
        k = n // 2 if h < 4 else n // 2 - 1
        q[h, [h - 1, k]] = q[h, [k, h - 1]]
    q[4, [0, 1, 2, n - 1, n - 2, n - 3]] = q[4, [n - 1, n - 2, n - 3, 0, 1, 2]]
    return q
def big(v):
    v = v.astype(np.float32)
    v[np.abs(v) < np.float32(2.0 ** -16)] = 0
    return v.astype(BF)
def numbers_of(rng):
    return {"x": big(f(rng, N, 128, 4 * C)), "u": np.array(f(rng, N, 128, 512)), "v": np.array(f(rng, N, 128, 512))}
def layers(rng, still=[]):
    w = (rng.random((N, 128, 2048)) * 2.0 - 1.0) * 0.054 * np.exp2(-rng.integers(0, 2, (N, 128, 1)))
    w = big(w).reshape(N, 8, 16, 4, 8, 16, 4)
    for i in still:
        w[:, :, i] = 0
        w[:, :, :, :, :, i] = 0
    return w
def weights(rng, w):
    c, p = packed(np.ascontiguousarray(w).reshape(N, 128, 2048), rng)
    return {"wc": c, "ws": p}
def setup_inputs(rng):
    return {**numbers_of(rng), **weights(rng, layers(rng))}
def setup_inputs_ties(rng):
    d = numbers_of(rng)
    x = d["x"].reshape(N, 8, 16, C, 4)
    x[:, :, 0] = 0
    x[:, :, 0, :, 0] = rng.integers(1, 4, (N, 8, C)).astype(np.float32).astype(BF)
    u = d["u"].reshape(N, 128, 128, 4)
    one = u[:, :, :1].copy()
    one[:, :8] = 0
    u[:, :, ::16] = 0
    o = rng.permutation(N)
    for r in range(N):
        if o[r] == 2:
            u[r, :, ::16] = one[r]
            s = mx_ref.matmul(mx_ref.quantize(np.ascontiguousarray(u[r].reshape(128, 512))), mx_ref.quantize(np.ascontiguousarray(x[r].reshape(128, 4 * C))))[0]
            x[r, 0, 0] = 0
            x[r, 0, 0, np.argsort(-s, kind="stable")[C // 2], 0] = 2.0
            u[r, 0, 0, 0] = -2.0 ** 20
        else:
            for h in range(0, 128, 16): u[r, h, h, 0] = 0.0 if o[r] == 0 else -1.0 if o[r] == 1 else 1.0
    return {"x": x.reshape(N, 128, 4 * C), "u": u.reshape(N, 128, 512), "v": d["v"], **weights(rng, layers(rng, [0]))}
def setup_inputs_near(rng):
    d = numbers_of(rng)
    x = d["x"].astype(np.float32).reshape(N, 8, 16, C, 4)
    u = d["u"].reshape(N, 128, 128, 4)
    x[:, :, 0] = 0
    x[:, :, 8:] = 0
    u[:, :, ::16] = 0
    o = rng.permutation(N) % 4
    for r in range(N):
        k = 1.0 if o[r] == 0 else 2.0 ** -30
        if o[r] < 2:
            x[r, :, 0, :, 0] = rng.integers(0, 2, (8, C)) * 2.0 - 1.0
            x[r, :, 11, :, 0] = 2.0 ** -10
        if o[r] == 2:
            e = np.argsort(rng.random((8, C)), axis=1)
            x[r, :, 0, :, 0] = np.where(e < C // 16, 1.0, np.where(e < C // 8, -1.0, 0.0))
        if o[r] < 3:
            s = rng.integers(0, 16, (8, C))
            x[r, :, 8] = ((s[:, :, None] >> np.arange(4)) & 1) * np.exp2(np.arange(4) - 23.0)
        else:
            a = rng.integers(0, 4, (8, C))
            x[r, :, 10, :, 0] = np.array([1.0, 0.0, -1.0, 0.0])[a] * 2.0 ** -27
            x[r, :, 10, :, 1] = np.array([0.0, 1.125, 1.125, 0.0])[a] * 2.0 ** -27
        for h in range(0, 128, 16):
            if o[r] < 2:
                u[r, h, h, 0] = k
                u[r, h + 11, h, 0] = k
            if o[r] == 2: u[r, h, h, 0] = 1.0
            if o[r] < 3: u[r, h + 8, h] = k
            else:
                u[r, h + 10, h, 0] = 1.25 * k
                u[r, h + 10, h, 1] = 1.125 * k
    return {"x": x.reshape(N, 128, 4 * C).astype(BF), "u": u.reshape(N, 128, 512), "v": d["v"], **weights(rng, layers(rng, [0, 8, 9, 10, 11, 12, 13, 14, 15]))}
def setup_inputs_odd(rng):
    d = numbers_of(rng)
    a = (1.0 + (2 * rng.integers(0, 64, (N, 8, 2, C, 32)) + 1) * 2.0 ** -7) * np.exp2(-rng.integers(8, 15, (N, 8, 2, C, 32))) * (rng.integers(0, 2, (N, 8, 2, C, 32)) * 2.0 - 1.0)
    e = rng.integers(0, 32, (N, 8, 2, C, 1))
    np.put_along_axis(a, e, 1.96875 * (rng.integers(0, 2, (N, 8, 2, C, 1)) * 2.0 - 1.0), axis=4)
    a *= np.exp2(rng.integers(-1, 3, (N, 8, 2, C, 1)))
    d["x"] = np.ascontiguousarray(a.reshape(N, 8, 2, C, 8, 4).transpose(0, 1, 2, 4, 3, 5)).reshape(N, 128, 4 * C).astype(np.float32).astype(BF)
    return {**d, **weights(rng, layers(rng))}
def setup_inputs_ends(rng):
    d = numbers_of(rng)
    e = rng.permutation(N)
    o = e % 4
    x = (0.9 + 0.1 * rng.random((N, 8, 16, C, 4))) * 2.0 ** 30
    x[:, :, 8:] = 2.0 ** -27 * (rng.integers(0, 2, (N, 8, 8, C, 4)) * 2.0 - 1.0)
    u, v = d["u"].reshape(N, 128, 128, 4), d["v"]
    w = np.zeros((N, 8, 16, 4, 8, 16, 4), np.float32)
    for r in range(N):
        a = np.zeros((8, 16, 8, 4))
        if o[r] == 0: x[r] = -2.0 ** 30 * (0.9 + 0.1 * rng.random((8, 16, C, 4)))
        if o[r] == 1: x[r, :, :8] *= rng.integers(0, 2, (1, 1, C, 1)) * 2.0 - 1.0
        if o[r] == 2: x[r, :, :8] *= rng.integers(0, 2, (8, 8, C, 4)) * 2.0 - 1.0
        if o[r] == 3:
            q = meet(C)[rng.permutation(8)] if e[r] == 3 else np.stack([C - 1 - np.arange(C)] * 8)
            x[r, :, :8] *= rng.integers(0, 2, (8, 1, C, 1)) * 2.0 - 1.0
            x[r, :, 0] = 0
            x[r, :, 0, :, :3] = (((C - 1 - q)[:, :, None] >> np.array([0, 3, 6])) & 7) * 2.0 ** 27
            for g in range(0 if e[r] == 3 else 4, 8): a[g, 0, g, :3] = 2.0 ** 20 * np.array([1.0, 8.0, 64.0])
        if o[r] == 0: a = 2.0 ** 30 * (1.0 - 0.1 * rng.random((8, 16, 8, 4)))
        if o[r] == 1:
            a[:, :8] = 2.0 ** 30 * (1.0 - 0.1 * rng.random((8, 8, 8, 4)))
            a *= (rng.permutation(8) % 2 * 2.0 - 1.0)[None, None, :, None]
        if o[r] == 2: a[:, 8:] = 2.0 ** -30 * (rng.integers(0, 2, (8, 8, 8, 4)) * 2.0 - 1.0)
        u[r, :, ::16] = a.reshape(128, 8, 4).astype(np.float32).astype(BF)
        if o[r] == 0: w[r, :, :8, :, :, :8] = 0.0546875
        if o[r] in (1, 3): w[r, :, :8, :, :, :8] = 0.0546875 * (rng.integers(0, 2, (8, 8, 4, 8, 8, 4)) * 2.0 - 1.0)
        if o[r] == 0: v[r] = 2.0 ** 30
        if o[r] == 1: v[r] = (2.0 ** 30 * (rng.integers(0, 2, (128, 512)) * 2.0 - 1.0)).astype(np.float32).astype(BF)
        if o[r] == 2: v[r] = (2.0 ** -30 * (rng.integers(0, 2, (128, 512)) * 2.0 - 1.0)).astype(np.float32).astype(BF)
    return {"x": x.astype(np.float32).reshape(N, 128, 4 * C).astype(BF), "u": u.reshape(N, 128, 512), "v": v, **weights(rng, w.astype(BF))}
def setup_inputs_spread(rng):
    d = setup_inputs(rng)
    d["x"] = big(wide(rng, N, 128, 4 * C, cols=6))
    return d
def check_inputs(d):
    b = []
    for k, low in (("x", 2.0 ** -27), ("u", 2.0 ** -30), ("v", 2.0 ** -30)):
        a = np.abs(d[k].astype(np.float32))
        if not (np.isfinite(a).all() and ((a == 0) | (a >= low) & (a <= 2.0 ** 30)).all()): b.append("a value of " + k)
    none, least, most = [emit(mx_ref.quantize(np.full((128, 16), k, np.float32).astype(BF)))[1][0, 0] for k in (0.0, 2.0 ** -16, 2.0 ** -5)]
    for r in range(N):
        if ((d["wc"][r] == 0x7F) | (d["wc"][r] == 0xFF)).any(): b.append("wc: a code that is no number")
        s = mx_ref.live(d["ws"][r])
        if ((s != none) & ((s < least) | (s > most))).any(): b.append("ws: a scale out of range")
        if not (np.abs(decode(pk(d["wc"][r], d["ws"][r]))) < 2.0 ** -4).all(): b.append("wc, ws: a number of W that isn't below 2**-4 in size")
    return b
def reference(x, u, v, wc, ws):
    qu = [mx_ref.quantize(u[r]) for r in range(N)]
    lay = [pk(wc[r], ws[r]) for r in range(N)]
    now = [x[r] for r in range(N)]
    l, own = [None] * N, [None] * N
    for t in range(R):
        y, z = [], []
        for r in range(N):
            q = mx_ref.quantize(now[r])
            d = decode(q).astype(BF)
            s = mx_ref.matmul(qu[r], q)[::16] + np.float32(0.0)
            o = np.argsort(-s, axis=1, kind="stable")
            place = np.argsort(o, axis=1, kind="stable")
            m = np.sort(place, axis=0)
            l[r] = np.where(place <= m[3], o[:, m[4]], o[:, m[3]])
            c = np.argsort(m[0] - m[7], kind="stable")[:M]
            own[r] = l[r][:, c]
            z.append(mx_ref.quantize(gcols(d, own[r])))
            y.append(((now[r].astype(np.float32) + gcols(d, l[r]).astype(np.float32)) * np.float32(0.5)).astype(BF))
        for r in range(N):
            came = z[(r - 1 - t) % N]
            h = tile([mx_ref.matmul(pick(lay[r], np.arange(128 * b, 128 * b + 128)), came) * np.float32(0.03125) for b in range(4)])
            first = np.full((8, C), M)
            np.minimum.at(first, (np.arange(8)[:, None], own[r]), np.arange(M)[None])
            now[r] = gcols(np.concatenate([y[r], h], axis=1), np.where(first < M, C + first, np.arange(C)[None]))
    y, ol = np.zeros((N, 128, C), np.float32), np.zeros((N, 8, C), np.float32)
    oc, osc = np.zeros((N, 128, 4 * C), np.uint8), np.zeros((N, 16, C), np.uint8)
    for r in range(N):
        q = mx_ref.quantize(now[r])
        y[r] = mx_ref.matmul(mx_ref.quantize(v[r]), q)
        ol[r] = l[r]
        oc[r], osc[r] = emit(q)
    return {"y": y, "ol": ol, "oc": oc, "osc": osc}

@@ -1,0 +1,458 @@
+from concourse.mybir import dt, AluOpType as A, ActivationFunctionType as F
+
+C, M, R, N = 384, 192, 3, 8
+BIG = 1.0e29
+RND = 402653184.0
+TILES = [(384, [23, 22, 21]), (320, [20, 19, 18, 17]), (256, [16, 15, 14, 13]), (192, [12, 11, 10, 9]), (128, [8, 7, 6, 5]), (128, [4, 3, 2, 1])]
+COFS = [0, 384, 704, 960, 1152, 1280]
+
+SCRATCH, PLACE = {}, {}
+for _n, _w, _d in [
+        ("xs", 1536, "bfloat16"), ("ub", 512, "bfloat16"), ("vb", 512, "bfloat16"),
+        ("kc", 2048, "bfloat16"), ("kj", 1024, "bfloat16"), ("eb", 2048, "bfloat16"), ("idn", 128, "bfloat16"), ("zer", 128, "bfloat16"),
+        ("ione", 384, "int32"), ("itwo", 384, "int32"), ("mask", 384, "float32"), ("mmin", 384, "float32"), ("dzr", 384, "float32"), ("dzs", 384, "float32"), ("ramp", 384, "float32"),
+        ("jrow", 384, "float32"), ("jrev", 384, "float32"), ("kval", 192, "float32"), ("iok", 192, "bfloat16"),
+        ("dst", 384, "float32"), ("sc", 384, "float32"), ("junk", 6624, "bfloat16"), ("ds", 384, "float32"), ("cm", 384, "float32"), ("cw", 384, "float32"),
+        ("hl", 96, "bfloat16"), ("exa", 768, "bfloat16"), ("ow", 384, "float32"), ("nx", 192, "float32"),
+        ("zd", 192, "bfloat16"), ("exb", 1536, "bfloat16"), ("kr", 384, "float32"), ("oht", 768, "bfloat16"), ("crm", 192, "float32"), ("crw", 192, "float32"),
+        ("lr", 384, "float32"), ("lm", 192, "float32"), ("sl", 192, "float32"), ("zt", 768, "bfloat16"),
+        ("lrr", 192, "bfloat16"), ("slm", 192, "bfloat16"), ("dj", 1056, "bfloat16"), ("dg", 192, "float32"), ("dd", 192, "float32"),
+        ("nw", 576, "float32"), ("nm", 384, "float32"), ("ns", 384, "float32"), ("lmy", 384, "float32"), ("sly", 384, "float32"), ("yo", 384, "float32"), ("olt", 384, "float32"),
+        ("t0", 384, "bfloat16"), ("t1", 384, "bfloat16"), ("t2", 384, "bfloat16"), ("t3", 384, "bfloat16"),
+        ("w0", 576, "float32"), ("w1", 576, "float32"), ("w2", 576, "float32"), ("w3", 576, "float32")]:
+    SCRATCH[_n] = ("sbuf", [128, _w], _d)
+    PLACE[_n] = (_n, 0, _w)
+for _b, _d, _l in [
+        ("cpk", "float32", [("pmf", 2), ("phf", 2), ("phx", 2), ("phy", 2), ("cqi", 24), ("cq", 24), ("kti", 12), ("kt", 12), ("ktp", 12), ("hfi", 4), ("jfi", 4), ("jf", 4), ("jh4", 4), ("jl4", 4),
+                            ("ufi", 8), ("gmi", 8), ("gm", 8)]),
+        ("ipk", "int32", [("pint", 2), ("pmi", 2), ("phi", 2)]),
+        ("fpk", "float32", [("rs", 24), ("rq", 24), ("rq2", 24), ("qw", 24), ("vh", 96), ("mn", 96), ("mx", 96), ("sa", 48), ("sb", 48), ("um", 144), ("aw", 24), ("bw", 24), ("sp", 24), ("kwa", 24),
+                            ("kw", 24), ("fw", 24), ("dw", 24), ("fd", 24), ("mw", 24), ("zc", 48), ("kg", 48), ("ra", 4), ("rr", 4), ("sls", 12), ("du", 12), ("tot", 12), ("df", 12), ("dx", 12),
+                            ("dy", 12), ("dz", 12)]),
+        ("uck", "uint16", [("u8", 8), ("hl48", 4)]),
+        ("upk", "uint16", [("qo", 24), ("mo", 24), ("cof", 12), ("lo", 12), ("off", 12), ("no", 24), ("lyo", 24)])]:
+    _o = 0
+    for _n, _w in _l:
+        PLACE[_n] = (_b, _o, _w)
+        _o += (_w + 7) // 8 * 8
+    SCRATCH[_b] = ("sbuf", [128, _o], _d)
+for _i in range(6):
+    SCRATCH["cb%d" % _i] = ("sbuf", [128, 4 * TILES[_i][0]], "bfloat16")
+    PLACE["cb%d" % _i] = ("cb%d" % _i, 0, 4 * TILES[_i][0])
+for _i in range(8):
+    SCRATCH["ps%d" % _i] = ("psum", [128, 512], "float32")
+    PLACE["ps%d" % _i] = ("ps%d" % _i, 0, 512)
+
+
+def _codes(name, n):
+    for k, d in (("q", "float8_e4m3fn_x4"), ("s", "uint8")):
+        SCRATCH[name + k] = ("sbuf", [128, n], d)
+        PLACE[name + k] = (name + k, 0, n)
+
+
+for _i in range(3):
+    _codes("z%d" % _i, M)
+    _codes("a%d" % _i, M)
+for _n, _w in [("x", C), ("u", 128), ("ur", 128), ("v", 128), ("k", 512), ("j", 256), ("e", 512), ("w", 512), ("c", 1408), ("b", 192), ("p", C), ("o", 192)]:
+    _codes("m" + _n, _w)
+SEMAPHORES = ["sv", "ss", "sp", "sg", "sent", "arr0", "arr1", "arr2"] + ["d%d" % i for i in range(24)]
+
+
+def builder(g, T):
+    eng = {"v": g.vector, "s": g.scalar, "p": g.tensor, "g": g, "y": g.sync}
+    cnt = {"v": 0, "s": 0, "p": 0, "g": 0}
+    know = {e: {} for e in eng}
+    acc, ndma = {}, [0]
+
+    def reg(r):
+        return (r[0], 0, 512, 1) if r[0][:2] == "ps" else r
+
+    def meet(a, b):
+        if a[1] >= b[2] or b[1] >= a[2]:
+            return False
+        return not (a[3] == b[3] and a[3] > 1 and (a[1] - b[1]) % a[3])
+
+    def sync(e, reads, writes, extra=()):
+        want = {}
+        k = know[e]
+
+        def need(sem, n, snap):
+            if k.get(sem, 0) < n and want.get(sem, (0, None))[0] < n:
+                want[sem] = (n, snap)
+        for kind, rs in (("r", reads), ("w", writes)):
+            for r in rs:
+                r = reg(r)
+                ps = r[0][:2] == "ps"
+                for (k2, r2, e2, sem, n, snap) in acc.get(r[0], []):
+                    if not meet(r, r2):
+                        continue
+                    if kind == "r" and k2 == "r" and not (ps and e != e2):
+                        continue
+                    if e == e2 and sem[0] == "s" and k2 == "r":
+                        continue
+                    if e == e2 == "p" and ps:
+                        continue
+                    need(sem, n, snap)
+        for sem, n in extra:
+            need(sem, n, {})
+        for sem in sorted(want, key=lambda s: -len(want[s][1])):
+            n, snap = want[sem]
+            if k.get(sem, 0) >= n:
+                continue
+            eng[e].wait_ge(T.sem[sem], n)
+            k[sem] = n
+            for s2 in snap:
+                if k.get(s2, 0) < snap[s2]:
+                    k[s2] = snap[s2]
+
+    def note(e, reads, writes, sem, n):
+        snap = dict(know[e])
+        for r in writes:
+            r = reg(r)
+            old = acc.get(r[0], [])
+            if r[3] == 1:
+                old = [o for o in old if not (o[1][1] >= r[1] and o[1][2] <= r[2])]
+            acc[r[0]] = old + [("w", r, e, sem, n, snap)]
+        for r in reads:
+            r = reg(r)
+            old = [o for o in acc.get(r[0], []) if not (o[0] == "r" and o[2] == e and o[3] == sem and o[1] == r)]
+            acc[r[0]] = old + [("r", r, e, sem, n, snap)]
+
+    def call(e, reads, writes, make, extra=()):
+        sync(e, reads, writes, extra)
+        cnt[e] += 1
+        make(eng[e]).then_inc(T.sem["s" + e], 1)
+        note(e, reads, writes, "s" + e, cnt[e])
+
+    def dma(e, reads, writes, out, in_):
+        sync(e, reads, writes)
+        sem = "d%d" % ndma[0]
+        ndma[0] += 1
+        eng[e].dma_start(out, in_).then_inc(T.sem[sem], 16)
+        note(e, reads, writes, sem, 16)
+
+    def send(reads, make):
+        sync("g", reads, [])
+        make()
+
+    def finish():
+        for e in ("v", "s", "p", "g"):
+            if cnt[e] and know["g"].get("s" + e, 0) < cnt[e]:
+                g.wait_ge(T.sem["s" + e], cnt[e])
+        for i in range(ndma[0]):
+            g.wait_ge(T.sem["d%d" % i], 16)
+    return call, dma, send, finish
+
+
+def rank_program(g, core, T, topo):
+    rank = T.rank_of(core)
+    if rank is None:
+        return
+    call, dma, send, finish = builder(g, T)
+
+    def V(name, lo=0, hi=None, st=1):
+        b, o, w = PLACE[name]
+        return (b, o + lo, o + (w if hi is None else hi), st)
+
+    def ap(r):
+        return T[r[0]][:, r[1]:r[2]] if r[3] == 1 else T[r[0]][:, r[1]:r[2]:r[3]]
+
+    def src(r, off):
+        return ap(r) if off is None else ap(r).indirect(ap(off))
+
+    def rd(*rs):
+        return [r for r in rs if isinstance(r, tuple)]
+
+    def val(s):
+        return ap(s) if isinstance(s, tuple) else s
+
+    def tt(out, a, b, op, off=None):
+        call("v", rd(a, b, off), [out], lambda e: e.tensor_tensor(ap(out), src(a, off), ap(b), op))
+
+    def ts(out, a, s1, op0, s2=None, op1=None, off=None):
+        if op1 is None:
+            call("v", rd(a, s1, off), [out], lambda e: e.tensor_scalar(ap(out), src(a, off), val(s1), None, op0))
+        else:
+            call("v", rd(a, s1, s2, off), [out], lambda e: e.tensor_scalar(ap(out), src(a, off), val(s1), val(s2), op0, op1))
+
+    def cp(out, a, off=None, ooff=None):
+        call("v", rd(a, off, ooff), [out], lambda e: e.tensor_copy(src(out, ooff), src(a, off)))
+
+    def ms(out, c):
+        call("v", [], [out], lambda e: e.memset(ap(out), c))
+
+    def scan(out, d0, d1, op0, op1):
+        call("v", [d0, d1], [out], lambda e: e.tensor_tensor_scan(ap(out), ap(d0), ap(d1), 0.0, op0, op1))
+
+    def act(out, a, func=F.Copy, scale=1.0, bias=0.0, accum=None, off=None):
+        kw = {}
+        if isinstance(scale, tuple) or scale != 1.0:
+            kw["scale"] = val(scale)
+        if isinstance(bias, tuple) or bias != 0.0:
+            kw["bias"] = val(bias)
+        if accum is not None:
+            kw["accum_out"] = ap(accum)
+        call("s", rd(a, scale, bias, off), [out] + rd(accum), lambda e: e.activation(ap(out), src(a, off), func, **kw))
+
+    def quant(q, lo, n, tile, tlo=0):
+        o, s, i = V(q + "q", lo, lo + n), V(q + "s", lo, lo + n), V(tile, tlo, tlo + 4 * n)
+        call("v", [i], [o, s], lambda e: e.quantize_mx(ap(o), ap(s), ap(i)))
+
+    def mm(ps, n, l, llo, r, rlo, start=True, stop=True, extra=()):
+        lc, lsc = V(l + "q", llo, llo + 128), V(l + "s", llo, llo + 128)
+        rc, rsc = V(r + "q", rlo, rlo + n), V(r + "s", rlo, rlo + n)
+        o = (ps, 0, n, 1)
+        call("p", [lc, lsc, rc, rsc], [o], lambda e: e.matmul_mx(ap(o), ap(lc), ap(lsc), ap(rc), ap(rsc), start, stop), extra)
+
+    def iota(out, pattern, base, cm):
+        if SCRATCH[out[0]][2] == "int32":
+            call("g", [], [out], lambda e: e.iota(ap(out), pattern, base, cm))
+        else:
+            call("g", [], [out], lambda e: e.iota(ap(out), pattern, base, cm, allow_small_or_imprecise_dtypes=True))
+
+    def select(out, a, pattern, op, fill, base, cm):
+        call("g", [a], [out], lambda e: e.affine_select(ap(out), ap(a), pattern, op, fill, base, cm))
+
+    dma("y", [], [V("ub")], T.ub[:], T.u[:])
+    dma("s", [], [V("xs")], T.xs[:], T.x[:])
+    dma("y", [], [V("mwq")], T.mwq[:].bitcast(dt.uint8), T.wc[:])
+    dma("y", [], [V("mws")], T.mws[:], T.ws[:])
+    dma("y", [], [V("vb")], T.vb[:], T.v[:])
+
+    iota(V("ufi"), [[16, 8]], 0, 0)
+    iota(V("pint"), [[0, 2]], 0, 1)
+    iota(V("ione"), [[1, 384]], 128, -1)
+    iota(V("ramp"), [[0, 24], [1, 16]], 0, 0)
+    cp(V("u8"), V("ufi"))
+    ms(V("kc", 512, 1024), -1.0)
+    ms(V("idn"), 1.0)
+    ms(V("rs"), 0.0)
+    for i, (n, cs) in enumerate(TILES):
+        ms(V("cb%d" % i, 64 * cs[-1], 4 * n), 0.0)
+    ms(V("kc", 1024, 1536), 0.0)
+    ms(V("kc", 1536, 2048), 512.0)
+    ts(V("phi"), V("pint"), 4, A.arith_shift_right)
+    cp(V("phf"), V("phi"))
+    ts(V("pmi"), V("pint"), 15, A.bitwise_and)
+    cp(V("pmf"), V("pmi"))
+    ts(V("itwo"), V("ione"), 15, A.bitwise_and)
+    ts(V("mask"), V("itwo"), 0, A.is_equal)
+    ts(V("dzr"), V("ramp"), 1.0, A.min)
+    ts(V("mmin"), V("mask"), 2 * BIG, A.mult, -BIG, A.add)
+    ts(V("dzs"), V("dzr"), 2 * BIG, A.mult, -BIG, A.add)
+    select(V("kc", 512, 1024), V("kc", 512, 1024), [[-16, 8], [0, 64]], A.is_ge, 0.0, 0, 1)
+    select(V("kc", 512, 1024), V("kc", 512, 1024), [[16, 8], [0, 64]], A.is_ge, 0.0, 15, -1)
+    select(V("idn"), V("idn"), [[-1, 128]], A.is_equal, 0.0, 0, 1)
+    iota(V("cqi"), [[-16, 24]], 383, 0)
+    iota(V("gmi"), [[1, 8]], 0, 0)
+    iota(V("jrow"), [[1, 384]], 1, 0)
+    iota(V("hfi"), [[1, 4]], 0, 0)
+    iota(V("jrev"), [[-1, 384]], 383, 0)
+    iota(V("jfi"), [[16, 4]], 0, 1)
+    iota(V("iok"), [[-1, 192]], 191, 0)
+    iota(V("kti"), [[16, 12]], 384, 0)
+    iota(V("kval"), [[1, 192]], 384, 0)
+    act(V("kc", 1024, 1536, 4), V("mask", 0, 128))
+    act(V("kc", 1025, 1536, 4), V("mask", 0, 128))
+    act(V("kc", 0, 512), V("kc", 512, 1024))
+    act(V("kc", 3, 512, 4), V("kc", 515, 1024, 4), scale=-1.0)
+    quant("mu", 0, 128, "ub")
+    o8 = V("u8")
+    call("v", [V("muq"), o8], [V("murq")], lambda e: e.tensor_copy(T.murq[:].bitcast(dt.uint32), T.muq[:].bitcast(dt.uint32).indirect(ap(o8))))
+    call("s", [V("mus"), o8], [V("murs")], lambda e: e.activation(T.murs[:], T.mus[:].indirect(ap(o8)), F.Copy))
+
+    def late_constants():
+        ms(V("eb"), 0.0)
+        for b in range(4):
+            act(V("eb", 512 * b + b, 512 * b + 512, 4), V("idn"))
+        ms(V("zer"), 0.0)
+        ms(V("hl"), 0.0)
+        ms(V("oht"), 0.0)
+        ms(V("du"), 0.0)
+        ms(V("zd"), 0.0)
+        ts(V("cq"), V("cqi"), V("pmf", 0, 1), A.subtract)
+        ts(V("gm"), V("gmi"), V("phf", 0, 1), A.is_equal)
+        ts(V("phx"), V("phf"), 3.0, A.mult)
+        ts(V("hl48"), V("hfi"), V("phx", 0, 1), A.add)
+        ts(V("phy"), V("phf"), 32.0, A.mult)
+        ts(V("jf"), V("jfi"), V("phy", 0, 1), A.add)
+        ts(V("jh4"), V("jf"), RND, A.add, RND, A.subtract)
+        tt(V("jl4"), V("jf"), V("jh4"), A.subtract)
+        ts(V("kt"), V("kti"), V("pmf", 0, 1), A.add)
+        ts(V("ktp"), V("kt"), 1.0, A.add)
+
+    def W16(name, n):
+        return V(name, 15, n, 16)
+
+    for t in range(R):
+        quant("mx", 0, C, "xs")
+        mm("ps0", C, "mur", 0, "mx", 0)
+        tt(V("dst"), V("ps0", 0, C), V("mmin"), A.min)
+        scan(V("sc"), V("dzs"), V("dst"), A.min, A.max)
+        jk = 0
+        for i, (n, cs) in enumerate(TILES):
+            cb = "cb%d" % i
+            if i == (4 if t == 0 else 0):
+                if t == 0:
+                    quant("me", 0, 512, "eb")
+                for b in range(4):
+                    mm("ps%d" % (1 + b), C, "me", 128 * b, "mx", 0)
+            for w, c in enumerate(cs):
+                ts(V(cb, w, 64 * c, 4), V("ps0", 0, 16 * c), V("sc", 16 * c + 15, 16 * c + 16), A.is_ge)
+            if i == 0:
+                tt(V(cb, 3, 4 * C, 4), V("ps0", 0, C), V("sc"), A.is_le)
+            quant("mc", COFS[i], n, cb)
+            if t == 0 and i == 0:
+                quant("mk", 0, 512, "kc")
+            mm("ps5", n, "mk", 0 if i == 0 else 128, "mc", COFS[i], i == 0, i == 5)
+            for w, c in enumerate(cs):
+                act(V("junk", jk, jk + 16 * c), V(cb, w, 64 * c, 4), accum=V("rs", c, c + 1))
+                jk += 16 * c
+            if t == 0 and i == 2:
+                late_constants()
+        scan(V("ds"), V("dzr"), V("cb0", 3, 4 * C, 4), A.mult, A.add)
+        tt(V("rq"), V("cq"), W16("ds", C), A.subtract)
+        tt(V("cm"), V("ps5", 0, C), V("mask"), A.mult)
+        scan(V("cw"), V("dzr"), V("cm"), A.mult, A.add)
+        tt(V("rq2"), V("rq"), V("rs"), A.add)
+        tt(V("qw"), V("rq2"), W16("cw", C), A.add)
+        ts(V("hl", 0, 96, 4), V("qw"), RND, A.add, RND, A.subtract)
+        tt(V("hl", 1, 96, 4), V("qw"), V("hl", 0, 96, 4), A.subtract)
+        cp(V("qo"), V("qw"))
+        for h in range(8):
+            o = V("exa", 96 * h, 96 * h + 96)
+            if h < 6:
+                ts(o, V("hl"), V("gm", h, h + 1), A.mult)
+            else:
+                act(o, V("hl"), scale=V("gm", h, h + 1))
+        quant("mb", 0, 192, "exa")
+        mm("ps6", 192, "mk", 256, "mb", 0)
+        cp(V("ow"), V("jrow"), ooff=V("qo"))
+        for b in range(4):
+            act(V("t%d" % b), V("ps%d" % (1 + b), 0, C))
+        cp(V("vh"), V("ps6", 96, 192))
+        tt(V("nx", 0, 192, 2), V("ps6", 0, 96), V("vh"), A.min)
+        tt(V("nx", 1, 192, 2), V("ps6", 0, 96), V("vh"), A.max)
+        tt(V("mn"), V("nx", 0, 96), V("nx", 96, 192), A.min)
+        tt(V("mx"), V("nx", 0, 96), V("nx", 96, 192), A.max)
+        tt(V("um", 0, 24), V("mn", 0, 48, 2), V("mn", 48, 96, 2), A.min)
+        tt(V("um", 24, 48), V("mx", 1, 48, 2), V("mx", 49, 96, 2), A.max)
+        tt(V("sp"), V("um", 24, 48), V("um", 0, 24), A.subtract)
+        tt(V("zc"), V("sp"), V("mask", 0, 48), A.mult, off=V("hl48", 0, 3))
+        ts(V("kwa"), V("sp"), 512.0, A.mult)
+        ts(V("zd", 0, 192, 4), V("zc"), RND, A.add, RND, A.subtract)
+        tt(V("kw"), V("kwa"), V("cq"), A.add)
+        tt(V("zd", 1, 192, 4), V("zc"), V("zd", 0, 192, 4), A.subtract)
+        for h in range(8):
+            o = V("exb", 192 * h, 192 * h + 192)
+            if h < 6:
+                ts(o, V("zd"), V("gm", h, h + 1), A.mult)
+            else:
+                act(o, V("zd"), scale=V("gm", h, h + 1))
+        cp(V("kg"), V("kw"), off=V("hl48", 0, 3))
+        quant("mp", 0, C, "exb")
+        mm("ps7", C, "mk", 384, "mp", 0)
+        tt(V("sa"), V("mx", 0, 96, 2), V("mn", 1, 96, 2), A.min)
+        tt(V("sb"), V("mx", 0, 96, 2), V("mn", 1, 96, 2), A.max)
+        tt(V("um", 48, 72), V("mn", 0, 48, 2), V("mn", 48, 96, 2), A.max)
+        tt(V("um", 72, 96), V("mx", 1, 48, 2), V("mx", 49, 96, 2), A.min)
+        tt(V("kr"), V("ps7", 0, C), V("jrev"), A.add)
+        for h in range(3):
+            act(V("junk", 5472 + 384 * h, 5856 + 384 * h), V("kr"), F.Sign, scale=-1.0, bias=V("kg", 16 * h, 16 * h + 1), accum=V("ra", h, h + 1))
+        tt(V("um", 96, 120), V("sb", 0, 24), V("sb", 24, 48), A.min)
+        tt(V("um", 120, 144), V("sa", 0, 24), V("sa", 24, 48), A.max)
+        tt(V("aw"), V("um", 48, 72), V("um", 96, 120), A.max)
+        tt(V("bw"), V("um", 72, 96), V("um", 120, 144), A.min)
+        tt(V("um", 0, 24), V("aw"), V("bw"), A.min)
+        tt(V("um", 24, 48), V("aw"), V("bw"), A.max)
+        tt(V("fw"), V("qw"), V("um", 0, 24), A.is_le)
+        tt(V("dw"), V("um", 24, 48), V("um", 0, 24), A.subtract)
+        tt(V("fd"), V("fw"), V("dw"), A.mult)
+        tt(V("mw"), V("fd"), V("um", 0, 24), A.add)
+        cp(V("mo"), V("mw"))
+        cp(V("lr"), V("ow"), off=V("mo"))
+        if t == 0:
+            for k in range(4):
+                ts(V("kj", k, 512, 4), V("zer"), V("jh4", k, k + 1), A.add)
+                ts(V("kj", 512 + k, 1024, 4), V("zer"), V("jl4", k, k + 1), A.add)
+            quant("mj", 0, 256, "kj")
+        ts(V("rr", 0, 3), V("ra", 0, 3), -0.5, A.mult, 191.5, A.add)
+        for h in range(3):
+            ts(V("oht", h, 768, 4), V("iok"), V("rr", h, h + 1), A.is_equal)
+        quant("mo", 0, 192, "oht")
+        mm("ps6", 192, "mj", 0, "mo", 0, True, False)
+        mm("ps6", 192, "mj", 128, "mo", 0, False, True)
+        tt(V("crm"), V("ps6", 0, M), V("mask", 0, M), A.mult)
+        scan(V("crw"), V("dzr", 0, M), V("crm"), A.mult, A.add)
+        cp(V("cof"), W16("crw", M))
+        tt(V("lm"), V("lr"), V("mask", 0, M), A.mult, off=V("cof"))
+        scan(V("sl"), V("dzr", 0, M), V("lm"), A.mult, A.add)
+        ts(V("lo"), W16("sl", M), -1.0, A.add)
+        for b in (2, 3):
+            act(V("zt", b, 768, 4), V("t%d" % b), off=V("lo"))
+        for b in (0, 1):
+            cp(V("zt", b, 768, 4), V("t%d" % b), off=V("lo"))
+        z, a = "z%d" % t, "a%d" % t
+        quant(z, 0, M, "zt")
+        dst = T.cores[(rank + 1 + t) % N]
+        rid, pid = topo.addr(dst)[:2]
+        mask = topo.mask(core, dst)
+        arr = T.sem["arr%d" % t]
+        send([V(z + "q")], lambda: g.remote_dma(T[a + "q"][:].bitcast(dt.uint8), T[z + "q"][:].bitcast(dt.uint8), arr, T.sem.sent, pid, rid, mask))
+        send([V(z + "s")], lambda: g.remote_dma(T[a + "s"][:], T[z + "s"][:], arr, T.sem.sent, pid, rid, mask))
+        iota(V("nw", 0, C), [[1, C]], 0, 0)
+        act(V("lrr"), V("lr"), F.Identity, bias=-192.0, off=V("cof"))
+        ts(V("sls"), W16("sl", M), -192.0, A.add)
+        ts(V("slm"), V("sl"), -192.0, A.add)
+        tt(V("lmy"), V("ow"), V("mask"), A.mult, off=V("mo"))
+        d = 0
+        for c in range(11):
+            n = M - 16 * (c + 1)
+            ts(V("dj", d, d + n), V("lrr", 16 * (c + 1), M), V("sls", c, c + 1), A.is_equal)
+            act(V("junk", 4416 + d, 4416 + d + n), V("dj", d, d + n), accum=V("du", c, c + 1))
+            d += n
+        tt(V("dg"), V("lrr"), V("slm"), A.is_equal)
+        scan(V("sly"), V("dzr"), V("lmy"), A.mult, A.add)
+        scan(V("dd"), V("dzr", 0, M), V("dg"), A.mult, A.add)
+        ts(V("lyo"), W16("sly", C), -1.0, A.add)
+        tt(V("dx"), W16("sl", M), V("ktp"), A.subtract)
+        tt(V("tot"), V("du"), W16("dd", M), A.add)
+        for b in range(4):
+            tt(V("w%d" % b, 0, C), V("t%d" % b), V("xs", b, 4 * C, 4), A.add, off=V("lyo"))
+            if b == 0:
+                ts(V("df"), V("tot"), 1.0, A.is_equal)
+                tt(V("dy"), V("df"), V("dx"), A.mult)
+                tt(V("dz"), V("dy"), V("kt"), A.add)
+                cp(V("off"), V("dz"))
+                cp(V("nw"), V("kval"), ooff=V("off"))
+                tt(V("nm"), V("nw", 0, C), V("mask"), A.mult)
+                scan(V("ns"), V("dzr"), V("nm"), A.mult, A.add)
+                cp(V("no"), W16("ns", C))
+        if t == R - 1:
+            act(V("olt"), V("lr"), F.Identity, bias=-1.0)
+            dma("y", [V("olt")], [], T.ol[:], T.olt[0:128:16, :])
+            quant("mv", 0, 128, "vb")
+        came = topo.engines(T.cores[(rank - 1 - t) % N], core)
+        for b in range(4):
+            mm("ps%d" % (1 + b), M, "mw", 128 * b, a, 0, extra=[("arr%d" % t, 2 * len(came))])
+        for b in range(4):
+            o = V("w%d" % b, C, C + M)
+            if b % 2 == 0:
+                ts(o, V("ps%d" % (1 + b), 0, M), 0.0625, A.mult)
+            else:
+                act(o, V("ps%d" % (1 + b), 0, M), scale=0.0625)
+        for b in range(4):
+            o = V("xs", b, 4 * C, 4)
+            if b % 2 == 0:
+                ts(o, V("w%d" % b), 0.5, A.mult, off=V("no"))
+            else:
+                act(o, V("w%d" % b), scale=0.5, off=V("no"))
+    quant("mx", 0, C, "xs")
+    mm("ps0", C, "mv", 0, "mx", 0)
+    dma("y", [V("mxq")], [], T.oc[:], T.mxq[:].bitcast(dt.uint8))
+    for k in range(4):
+        dma("y", [V("mxs")], [], T.osc[4 * k:4 * k + 4, :], T.mxs[32 * k:32 * k + 4, :])
+    act(V("yo"), V("ps0", 0, C))
+    dma("s", [V("yo")], [], T.y[:], T.yo[:])
+    finish()
+    g.wait_ge(T.sem.sent, sum(2 * len(topo.engines(core, T.cores[(rank + 1 + t) % N])) for t in range(R)))

@@ -1,33 +1,37 @@
-from concourse.mybir import dt, AluOpType as A, ActivationFunctionType as F
+from concourse.mybir import dt, AluOpType as A, AxisListType, ActivationFunctionType as F
 
 C, M, R, N = 384, 192, 3, 8
+DA, DB = 6, 4
+DR, DE = 2, 9
+DG = 3
 BIG = 1.0e29
 RND = 402653184.0
 TILES = [(384, [23, 22, 21]), (320, [20, 19, 18, 17]), (256, [16, 15, 14, 13]), (192, [12, 11, 10, 9]), (128, [8, 7, 6, 5]), (128, [4, 3, 2, 1])]
 COFS = [0, 384, 704, 960, 1152, 1280]
+PACKS = {0: 0, 1: 1, 3: 2, 5: 4}
 
 SCRATCH, PLACE = {}, {}
 for _n, _w, _d in [
         ("xs", 1536, "bfloat16"), ("ub", 512, "bfloat16"), ("vb", 512, "bfloat16"),
         ("kc", 2048, "bfloat16"), ("kj", 1024, "bfloat16"), ("eb", 2048, "bfloat16"), ("idn", 128, "bfloat16"), ("zer", 128, "bfloat16"),
         ("ione", 384, "int32"), ("itwo", 384, "int32"), ("mask", 384, "float32"), ("mmin", 384, "float32"), ("dzr", 384, "float32"), ("dzs", 384, "float32"), ("ramp", 384, "float32"),
-        ("jrow", 384, "float32"), ("jrev", 384, "float32"), ("kval", 192, "float32"), ("iok", 192, "bfloat16"),
-        ("dst", 384, "float32"), ("sc", 384, "float32"), ("junk", 6624, "bfloat16"), ("ds", 384, "float32"), ("cm", 384, "float32"), ("cw", 384, "float32"),
+        ("jrow", 384, "float32"), ("jrev", 384, "float32"), ("kval", 192, "float32"), ("iok", 192, "bfloat16"), ("mske", 384, "float32"),
+        ("dst", 384, "float32"), ("sc", 384, "float32"), ("junk", 6624, "bfloat16"), ("ds", 384, "float32"), ("cm", 384, "float32"), ("cw", 384, "float32"), ("cb", 5632, "bfloat16"),
         ("hl", 96, "bfloat16"), ("exa", 768, "bfloat16"), ("ow", 384, "float32"), ("nx", 192, "float32"),
         ("zd", 192, "bfloat16"), ("exb", 1536, "bfloat16"), ("kr", 384, "float32"), ("oht", 768, "bfloat16"), ("crm", 192, "float32"), ("crw", 192, "float32"),
         ("lr", 384, "float32"), ("lm", 192, "float32"), ("sl", 192, "float32"), ("zt", 768, "bfloat16"),
-        ("lrr", 192, "bfloat16"), ("slm", 192, "bfloat16"), ("dj", 1056, "bfloat16"), ("dg", 192, "float32"), ("dd", 192, "float32"),
-        ("nw", 576, "float32"), ("nm", 384, "float32"), ("ns", 384, "float32"), ("lmy", 384, "float32"), ("sly", 384, "float32"), ("yo", 384, "float32"), ("olt", 384, "float32"),
+        ("lrr", 192, "bfloat16"), ("dj", 1056, "bfloat16"), ("dg", 192, "float32"), ("dd", 192, "float32"), ("kvm", 192, "float32"),
+        ("nw", 584, "float32"), ("ns", 384, "float32"), ("lmy", 384, "float32"), ("sly", 384, "float32"), ("yo", 384, "float32"), ("olt", 384, "float32"),
         ("t0", 384, "bfloat16"), ("t1", 384, "bfloat16"), ("t2", 384, "bfloat16"), ("t3", 384, "bfloat16"),
         ("w0", 576, "float32"), ("w1", 576, "float32"), ("w2", 576, "float32"), ("w3", 576, "float32")]:
     SCRATCH[_n] = ("sbuf", [128, _w], _d)
     PLACE[_n] = (_n, 0, _w)
 for _b, _d, _l in [
-        ("cpk", "float32", [("pmf", 2), ("phf", 2), ("phx", 2), ("phy", 2), ("cqi", 24), ("cq", 24), ("kti", 12), ("kt", 12), ("ktp", 12), ("hfi", 4), ("jfi", 4), ("jf", 4), ("jh4", 4), ("jl4", 4),
+        ("cpk", "float32", [("pmf", 2), ("phf", 2), ("phx", 2), ("phy", 2), ("cqi", 24), ("cq", 24), ("kti", 12), ("ktp", 12), ("hfi", 4), ("jfi", 4), ("jf", 4), ("jh4", 4), ("jl4", 4),
                             ("ufi", 8), ("gmi", 8), ("gm", 8)]),
         ("ipk", "int32", [("pint", 2), ("pmi", 2), ("phi", 2)]),
         ("fpk", "float32", [("rs", 24), ("rq", 24), ("rq2", 24), ("qw", 24), ("vh", 96), ("mn", 96), ("mx", 96), ("sa", 48), ("sb", 48), ("um", 144), ("aw", 24), ("bw", 24), ("sp", 24), ("kwa", 24),
-                            ("kw", 24), ("fw", 24), ("dw", 24), ("fd", 24), ("mw", 24), ("zc", 48), ("kg", 48), ("ra", 4), ("rr", 4), ("sls", 12), ("du", 12), ("tot", 12), ("df", 12), ("dx", 12),
+                            ("kw", 24), ("fw", 24), ("dw", 24), ("fd", 24), ("mw", 24), ("zc", 48), ("kg", 48), ("ra", 4), ("rr", 4), ("sls", 12), ("du", 12), ("tot", 12), ("df", 12),
                             ("dy", 12), ("dz", 12)]),
         ("uck", "uint16", [("u8", 8), ("hl48", 4)]),
         ("upk", "uint16", [("qo", 24), ("mo", 24), ("cof", 12), ("lo", 12), ("off", 12), ("no", 24), ("lyo", 24)])]:
@@ -36,9 +40,6 @@ for _b, _d, _l in [
         PLACE[_n] = (_b, _o, _w)
         _o += (_w + 7) // 8 * 8
     SCRATCH[_b] = ("sbuf", [128, _o], _d)
-for _i in range(6):
-    SCRATCH["cb%d" % _i] = ("sbuf", [128, 4 * TILES[_i][0]], "bfloat16")
-    PLACE["cb%d" % _i] = ("cb%d" % _i, 0, 4 * TILES[_i][0])
 for _i in range(8):
     SCRATCH["ps%d" % _i] = ("psum", [128, 512], "float32")
     PLACE["ps%d" % _i] = ("ps%d" % _i, 0, 512)
@@ -154,6 +155,9 @@ def rank_program(g, core, T, topo):
         b, o, w = PLACE[name]
         return (b, o + lo, o + (w if hi is None else hi), st)
 
+    def W16(name, n):
+        return V(name, 15, n, 16)
+
     def ap(r):
         return T[r[0]][:, r[1]:r[2]] if r[3] == 1 else T[r[0]][:, r[1]:r[2]:r[3]]
 
@@ -180,6 +184,9 @@ def rank_program(g, core, T, topo):
 
     def ms(out, c):
         call("v", [], [out], lambda e: e.memset(ap(out), c))
+
+    def sumup(out, a):
+        call("v", [a], [out], lambda e: e.tensor_reduce(ap(out), ap(a), AxisListType.X, A.add))
 
     def scan(out, d0, d1, op0, op1):
         call("v", [d0, d1], [out], lambda e: e.tensor_tensor_scan(ap(out), ap(d0), ap(d1), 0.0, op0, op1))
@@ -213,6 +220,17 @@ def rank_program(g, core, T, topo):
     def select(out, a, pattern, op, fill, base, cm):
         call("g", [a], [out], lambda e: e.affine_select(ap(out), ap(a), pattern, op, fill, base, cm))
 
+    def expand(out, w, a, dv):
+        for h in range(7, -1, -1):
+            o = V(out, w * h, w * h + w)
+            if h < dv:
+                ts(o, V(a), V("gm", h, h + 1), A.mult)
+            else:
+                act(o, V(a), scale=V("gm", h, h + 1))
+
+    def half(b):
+        tt(V("w%d" % b, 0, C), V("t%d" % b), V("xs", b, 4 * C, 4), A.add, off=V("lyo"))
+
     dma("y", [], [V("ub")], T.ub[:], T.u[:])
     dma("s", [], [V("xs")], T.xs[:], T.x[:])
     dma("y", [], [V("mwq")], T.mwq[:].bitcast(dt.uint8), T.wc[:])
@@ -227,22 +245,28 @@ def rank_program(g, core, T, topo):
     ms(V("kc", 512, 1024), -1.0)
     ms(V("idn"), 1.0)
     ms(V("rs"), 0.0)
-    for i, (n, cs) in enumerate(TILES):
-        ms(V("cb%d" % i, 64 * cs[-1], 4 * n), 0.0)
-    ms(V("kc", 1024, 1536), 0.0)
-    ms(V("kc", 1536, 2048), 512.0)
     ts(V("phi"), V("pint"), 4, A.arith_shift_right)
-    cp(V("phf"), V("phi"))
     ts(V("pmi"), V("pint"), 15, A.bitwise_and)
+    cp(V("phf"), V("phi"))
     cp(V("pmf"), V("pmi"))
     ts(V("itwo"), V("ione"), 15, A.bitwise_and)
     ts(V("mask"), V("itwo"), 0, A.is_equal)
     ts(V("dzr"), V("ramp"), 1.0, A.min)
-    ts(V("mmin"), V("mask"), 2 * BIG, A.mult, -BIG, A.add)
-    ts(V("dzs"), V("dzr"), 2 * BIG, A.mult, -BIG, A.add)
+    act(V("mmin"), V("mask"), F.Identity, scale=2 * BIG, bias=-BIG)
+    act(V("dzs"), V("dzr"), F.Identity, scale=2 * BIG, bias=-BIG)
+    quant("mu", 0, 128, "ub")
+    o8 = V("u8")
+    call("v", [V("muq"), o8], [V("murq")], lambda e: e.tensor_copy(T.murq[:].bitcast(dt.uint32), T.muq[:].bitcast(dt.uint32).indirect(ap(o8))))
+    call("s", [V("mus"), o8], [V("murs")], lambda e: e.activation(T.murs[:], T.mus[:].indirect(ap(o8)), F.Copy))
+    quant("mx", 0, C, "xs")
+    for i, (n, cs) in enumerate(TILES):
+        ms(V("cb", 4 * COFS[i] + 64 * cs[-1], 4 * (COFS[i] + n)), 0.0)
+    ms(V("kc", 1024, 1536), 0.0)
+    ms(V("kc", 1536, 2048), 512.0)
     select(V("kc", 512, 1024), V("kc", 512, 1024), [[-16, 8], [0, 64]], A.is_ge, 0.0, 0, 1)
     select(V("kc", 512, 1024), V("kc", 512, 1024), [[16, 8], [0, 64]], A.is_ge, 0.0, 15, -1)
     select(V("idn"), V("idn"), [[-1, 128]], A.is_equal, 0.0, 0, 1)
+    iota(V("eb"), [[0, 2048]], 0, 0)
     iota(V("cqi"), [[-16, 24]], 383, 0)
     iota(V("gmi"), [[1, 8]], 0, 0)
     iota(V("jrow"), [[1, 384]], 1, 0)
@@ -250,24 +274,19 @@ def rank_program(g, core, T, topo):
     iota(V("jrev"), [[-1, 384]], 383, 0)
     iota(V("jfi"), [[16, 4]], 0, 1)
     iota(V("iok"), [[-1, 192]], 191, 0)
-    iota(V("kti"), [[16, 12]], 384, 0)
+    iota(V("kti"), [[16, 12]], 385, 0)
     iota(V("kval"), [[1, 192]], 384, 0)
+    iota(V("oht"), [[0, 768]], 0, 0)
     act(V("kc", 1024, 1536, 4), V("mask", 0, 128))
     act(V("kc", 1025, 1536, 4), V("mask", 0, 128))
     act(V("kc", 0, 512), V("kc", 512, 1024))
     act(V("kc", 3, 512, 4), V("kc", 515, 1024, 4), scale=-1.0)
-    quant("mu", 0, 128, "ub")
-    o8 = V("u8")
-    call("v", [V("muq"), o8], [V("murq")], lambda e: e.tensor_copy(T.murq[:].bitcast(dt.uint32), T.muq[:].bitcast(dt.uint32).indirect(ap(o8))))
-    call("s", [V("mus"), o8], [V("murs")], lambda e: e.activation(T.murs[:], T.mus[:].indirect(ap(o8)), F.Copy))
 
     def late_constants():
-        ms(V("eb"), 0.0)
         for b in range(4):
             act(V("eb", 512 * b + b, 512 * b + 512, 4), V("idn"))
         ms(V("zer"), 0.0)
         ms(V("hl"), 0.0)
-        ms(V("oht"), 0.0)
         ms(V("du"), 0.0)
         ms(V("zd"), 0.0)
         ts(V("cq"), V("cqi"), V("pmf", 0, 1), A.subtract)
@@ -278,39 +297,45 @@ def rank_program(g, core, T, topo):
         ts(V("jf"), V("jfi"), V("phy", 0, 1), A.add)
         ts(V("jh4"), V("jf"), RND, A.add, RND, A.subtract)
         tt(V("jl4"), V("jf"), V("jh4"), A.subtract)
-        ts(V("kt"), V("kti"), V("pmf", 0, 1), A.add)
-        ts(V("ktp"), V("kt"), 1.0, A.add)
-
-    def W16(name, n):
-        return V(name, 15, n, 16)
+        ts(V("ktp"), V("kti"), V("pmf", 0, 1), A.add)
+        ts(V("mske"), V("jrow"), 1.0, A.subtract)
+        tt(V("mske"), V("mske"), V("mask"), A.mult)
 
     for t in range(R):
-        quant("mx", 0, C, "xs")
+        if t:
+            quant("mx", 0, C, "xs")
         mm("ps0", C, "mur", 0, "mx", 0)
         tt(V("dst"), V("ps0", 0, C), V("mmin"), A.min)
         scan(V("sc"), V("dzs"), V("dst"), A.min, A.max)
         jk = 0
         for i, (n, cs) in enumerate(TILES):
-            cb = "cb%d" % i
+            o = 4 * COFS[i]
             if i == (4 if t == 0 else 0):
                 if t == 0:
                     quant("me", 0, 512, "eb")
                 for b in range(4):
                     mm("ps%d" % (1 + b), C, "me", 128 * b, "mx", 0)
             for w, c in enumerate(cs):
-                ts(V(cb, w, 64 * c, 4), V("ps0", 0, 16 * c), V("sc", 16 * c + 15, 16 * c + 16), A.is_ge)
+                ts(V("cb", o + w, o + 64 * c, 4), V("ps0", 0, 16 * c), V("sc", 16 * c + 15, 16 * c + 16), A.is_ge)
             if i == 0:
-                tt(V(cb, 3, 4 * C, 4), V("ps0", 0, C), V("sc"), A.is_le)
-            quant("mc", COFS[i], n, cb)
-            if t == 0 and i == 0:
-                quant("mk", 0, 512, "kc")
-            mm("ps5", n, "mk", 0 if i == 0 else 128, "mc", COFS[i], i == 0, i == 5)
+                tt(V("cb", 3, 4 * C, 4), V("ps0", 0, C), V("sc"), A.is_le)
             for w, c in enumerate(cs):
-                act(V("junk", jk, jk + 16 * c), V(cb, w, 64 * c, 4), accum=V("rs", c, c + 1))
-                jk += 16 * c
-            if t == 0 and i == 2:
+                if c > DR:
+                    act(V("junk", jk, jk + 16 * c), V("cb", o + w, o + 64 * c, 4), accum=V("rs", c, c + 1))
+                    jk += 16 * c
+            if i in PACKS:
+                k = PACKS[i]
+                quant("mc", COFS[k], COFS[i] + n - COFS[k], "cb", 4 * COFS[k])
+                if t == 0 and i == 0:
+                    quant("mk", 0, 512, "kc")
+                for k in range(k, i + 1):
+                    mm("ps5", TILES[k][0], "mk", 0 if k == 0 else 128, "mc", COFS[k], k == 0, k == 5)
+            if t == 0 and i == 1:
                 late_constants()
-        scan(V("ds"), V("dzr"), V("cb0", 3, 4 * C, 4), A.mult, A.add)
+        for w, c in enumerate(TILES[5][1]):
+            if c <= DR:
+                sumup(V("rs", c, c + 1), V("cb", 4 * COFS[5] + w, 4 * COFS[5] + 64 * c, 4))
+        scan(V("ds"), V("dzr"), V("cb", 3, 4 * C, 4), A.mult, A.add)
         tt(V("rq"), V("cq"), W16("ds", C), A.subtract)
         tt(V("cm"), V("ps5", 0, C), V("mask"), A.mult)
         scan(V("cw"), V("dzr"), V("cm"), A.mult, A.add)
@@ -318,18 +343,17 @@ def rank_program(g, core, T, topo):
         tt(V("qw"), V("rq2"), W16("cw", C), A.add)
         ts(V("hl", 0, 96, 4), V("qw"), RND, A.add, RND, A.subtract)
         tt(V("hl", 1, 96, 4), V("qw"), V("hl", 0, 96, 4), A.subtract)
-        cp(V("qo"), V("qw"))
-        for h in range(8):
-            o = V("exa", 96 * h, 96 * h + 96)
-            if h < 6:
-                ts(o, V("hl"), V("gm", h, h + 1), A.mult)
-            else:
-                act(o, V("hl"), scale=V("gm", h, h + 1))
+        expand("exa", 96, "hl", DA)
         quant("mb", 0, 192, "exa")
         mm("ps6", 192, "mk", 256, "mb", 0)
+        cp(V("qo"), V("qw"))
         cp(V("ow"), V("jrow"), ooff=V("qo"))
         for b in range(4):
             act(V("t%d" % b), V("ps%d" % (1 + b), 0, C))
+        act(V("nw", 1, C + 1), V("mske"))
+        if t == 0:
+            for k in range(4):
+                act(V("kj", k, 512, 4), V("zer"), F.Identity, bias=V("jh4", k, k + 1))
         cp(V("vh"), V("ps6", 96, 192))
         tt(V("nx", 0, 192, 2), V("ps6", 0, 96), V("vh"), A.min)
         tt(V("nx", 1, 192, 2), V("ps6", 0, 96), V("vh"), A.max)
@@ -339,49 +363,48 @@ def rank_program(g, core, T, topo):
         tt(V("um", 24, 48), V("mx", 1, 48, 2), V("mx", 49, 96, 2), A.max)
         tt(V("sp"), V("um", 24, 48), V("um", 0, 24), A.subtract)
         tt(V("zc"), V("sp"), V("mask", 0, 48), A.mult, off=V("hl48", 0, 3))
-        ts(V("kwa"), V("sp"), 512.0, A.mult)
         ts(V("zd", 0, 192, 4), V("zc"), RND, A.add, RND, A.subtract)
-        tt(V("kw"), V("kwa"), V("cq"), A.add)
+        ts(V("kwa"), V("sp"), 512.0, A.mult)
         tt(V("zd", 1, 192, 4), V("zc"), V("zd", 0, 192, 4), A.subtract)
-        for h in range(8):
-            o = V("exb", 192 * h, 192 * h + 192)
-            if h < 6:
-                ts(o, V("zd"), V("gm", h, h + 1), A.mult)
-            else:
-                act(o, V("zd"), scale=V("gm", h, h + 1))
+        tt(V("kw"), V("kwa"), V("cq"), A.add)
+        expand("exb", 192, "zd", DB)
         cp(V("kg"), V("kw"), off=V("hl48", 0, 3))
-        quant("mp", 0, C, "exb")
-        mm("ps7", C, "mk", 384, "mp", 0)
         tt(V("sa"), V("mx", 0, 96, 2), V("mn", 1, 96, 2), A.min)
         tt(V("sb"), V("mx", 0, 96, 2), V("mn", 1, 96, 2), A.max)
         tt(V("um", 48, 72), V("mn", 0, 48, 2), V("mn", 48, 96, 2), A.max)
         tt(V("um", 72, 96), V("mx", 1, 48, 2), V("mx", 49, 96, 2), A.min)
-        tt(V("kr"), V("ps7", 0, C), V("jrev"), A.add)
-        for h in range(3):
-            act(V("junk", 5472 + 384 * h, 5856 + 384 * h), V("kr"), F.Sign, scale=-1.0, bias=V("kg", 16 * h, 16 * h + 1), accum=V("ra", h, h + 1))
         tt(V("um", 96, 120), V("sb", 0, 24), V("sb", 24, 48), A.min)
         tt(V("um", 120, 144), V("sa", 0, 24), V("sa", 24, 48), A.max)
         tt(V("aw"), V("um", 48, 72), V("um", 96, 120), A.max)
         tt(V("bw"), V("um", 72, 96), V("um", 120, 144), A.min)
+        quant("mp", 0, C, "exb")
+        mm("ps7", C, "mk", 384, "mp", 0)
         tt(V("um", 0, 24), V("aw"), V("bw"), A.min)
         tt(V("um", 24, 48), V("aw"), V("bw"), A.max)
         tt(V("fw"), V("qw"), V("um", 0, 24), A.is_le)
         tt(V("dw"), V("um", 24, 48), V("um", 0, 24), A.subtract)
         tt(V("fd"), V("fw"), V("dw"), A.mult)
         tt(V("mw"), V("fd"), V("um", 0, 24), A.add)
+        tt(V("kr"), V("ps7", 0, C), V("jrev"), A.add)
+        for h in range(3):
+            act(V("junk", 5472 + 384 * h, 5856 + 384 * h), V("kr"), F.Sign, scale=-1.0, bias=V("kg", 16 * h, 16 * h + 1), accum=V("ra", h, h + 1))
+        act(V("rr", 0, 3), V("ra", 0, 3), F.Identity, scale=-0.5, bias=191.5)
         cp(V("mo"), V("mw"))
-        cp(V("lr"), V("ow"), off=V("mo"))
+        act(V("lr"), V("ow"), off=V("mo"))
+        tt(V("lmy"), V("ow"), V("mask"), A.mult, off=V("mo"))
+        scan(V("sly"), V("dzr"), V("lmy"), A.mult, A.add)
+        ts(V("lyo"), W16("sly", C), -1.0, A.add)
+        half(0)
         if t == 0:
             for k in range(4):
-                ts(V("kj", k, 512, 4), V("zer"), V("jh4", k, k + 1), A.add)
                 ts(V("kj", 512 + k, 1024, 4), V("zer"), V("jl4", k, k + 1), A.add)
             quant("mj", 0, 256, "kj")
-        ts(V("rr", 0, 3), V("ra", 0, 3), -0.5, A.mult, 191.5, A.add)
         for h in range(3):
             ts(V("oht", h, 768, 4), V("iok"), V("rr", h, h + 1), A.is_equal)
         quant("mo", 0, 192, "oht")
         mm("ps6", 192, "mj", 0, "mo", 0, True, False)
         mm("ps6", 192, "mj", 128, "mo", 0, False, True)
+        half(1)
         tt(V("crm"), V("ps6", 0, M), V("mask", 0, M), A.mult)
         scan(V("crw"), V("dzr", 0, M), V("crm"), A.mult, A.add)
         cp(V("cof"), W16("crw", M))
@@ -393,6 +416,8 @@ def rank_program(g, core, T, topo):
         for b in (0, 1):
             cp(V("zt", b, 768, 4), V("t%d" % b), off=V("lo"))
         z, a = "z%d" % t, "a%d" % t
+        ts(V("sls"), W16("sl", M), -192.0, A.add)
+        tt(V("kvm"), V("mask"), V("kval"), A.mult, off=V("lo"))
         quant(z, 0, M, "zt")
         dst = T.cores[(rank + 1 + t) % N]
         rid, pid = topo.addr(dst)[:2]
@@ -400,34 +425,28 @@ def rank_program(g, core, T, topo):
         arr = T.sem["arr%d" % t]
         send([V(z + "q")], lambda: g.remote_dma(T[a + "q"][:].bitcast(dt.uint8), T[z + "q"][:].bitcast(dt.uint8), arr, T.sem.sent, pid, rid, mask))
         send([V(z + "s")], lambda: g.remote_dma(T[a + "s"][:], T[z + "s"][:], arr, T.sem.sent, pid, rid, mask))
-        iota(V("nw", 0, C), [[1, C]], 0, 0)
         act(V("lrr"), V("lr"), F.Identity, bias=-192.0, off=V("cof"))
-        ts(V("sls"), W16("sl", M), -192.0, A.add)
-        ts(V("slm"), V("sl"), -192.0, A.add)
-        tt(V("lmy"), V("ow"), V("mask"), A.mult, off=V("mo"))
         d = 0
         for c in range(11):
             n = M - 16 * (c + 1)
             ts(V("dj", d, d + n), V("lrr", 16 * (c + 1), M), V("sls", c, c + 1), A.is_equal)
-            act(V("junk", 4416 + d, 4416 + d + n), V("dj", d, d + n), accum=V("du", c, c + 1))
+            if c < DE:
+                act(V("junk", 4416 + d, 4416 + d + n), V("dj", d, d + n), accum=V("du", c, c + 1))
+            else:
+                sumup(V("du", c, c + 1), V("dj", d, d + n))
             d += n
-        tt(V("dg"), V("lrr"), V("slm"), A.is_equal)
-        scan(V("sly"), V("dzr"), V("lmy"), A.mult, A.add)
+        tt(V("dg"), V("lr"), V("sl"), A.is_equal, off=V("cof"))
         scan(V("dd"), V("dzr", 0, M), V("dg"), A.mult, A.add)
-        ts(V("lyo"), W16("sly", C), -1.0, A.add)
-        tt(V("dx"), W16("sl", M), V("ktp"), A.subtract)
+        half(2)
+        half(3)
         tt(V("tot"), V("du"), W16("dd", M), A.add)
-        for b in range(4):
-            tt(V("w%d" % b, 0, C), V("t%d" % b), V("xs", b, 4 * C, 4), A.add, off=V("lyo"))
-            if b == 0:
-                ts(V("df"), V("tot"), 1.0, A.is_equal)
-                tt(V("dy"), V("df"), V("dx"), A.mult)
-                tt(V("dz"), V("dy"), V("kt"), A.add)
-                cp(V("off"), V("dz"))
-                cp(V("nw"), V("kval"), ooff=V("off"))
-                tt(V("nm"), V("nw", 0, C), V("mask"), A.mult)
-                scan(V("ns"), V("dzr"), V("nm"), A.mult, A.add)
-                cp(V("no"), W16("ns", C))
+        ts(V("df"), V("tot"), 1.0, A.subtract, 1.0, A.min)
+        tt(V("dy"), V("df"), V("ktp"), A.mult)
+        tt(V("dz"), V("dy"), W16("sl", M), A.max)
+        cp(V("off"), V("dz"))
+        cp(V("nw"), V("kvm"), ooff=V("off"))
+        scan(V("ns"), V("dzr"), V("nw", 1, C + 1), A.mult, A.add)
+        cp(V("no"), W16("ns", C))
         if t == R - 1:
             act(V("olt"), V("lr"), F.Identity, bias=-1.0)
             dma("y", [V("olt")], [], T.ol[:], T.olt[0:128:16, :])
@@ -436,14 +455,10 @@ def rank_program(g, core, T, topo):
         for b in range(4):
             mm("ps%d" % (1 + b), M, "mw", 128 * b, a, 0, extra=[("arr%d" % t, 2 * len(came))])
         for b in range(4):
-            o = V("w%d" % b, C, C + M)
-            if b % 2 == 0:
-                ts(o, V("ps%d" % (1 + b), 0, M), 0.0625, A.mult)
-            else:
-                act(o, V("ps%d" % (1 + b), 0, M), scale=0.0625)
+            act(V("w%d" % b, C, C + M), V("ps%d" % (1 + b), 0, M), scale=0.0625)
         for b in range(4):
             o = V("xs", b, 4 * C, 4)
-            if b % 2 == 0:
+            if b < DG:
                 ts(o, V("w%d" % b), 0.5, A.mult, off=V("no"))
             else:
                 act(o, V("w%d" % b), scale=0.5, off=V("no"))

@@ -1,7 +1,7 @@
 from concourse.mybir import dt, AluOpType as A, AxisListType, ActivationFunctionType as F
 
 C, M, R, N = 384, 192, 3, 8
-DA, DB = 6, 4
+DA = 6
 DR, DE = 2, 9
 DG = 3
 BIG = 1.0e29
@@ -13,12 +13,12 @@ PACKS = {0: 0, 1: 1, 3: 2, 5: 4}
 SCRATCH, PLACE = {}, {}
 for _n, _w, _d in [
         ("xs", 1536, "bfloat16"), ("ub", 512, "bfloat16"), ("vb", 512, "bfloat16"),
-        ("kc", 2048, "bfloat16"), ("kj", 1024, "bfloat16"), ("eb", 2048, "bfloat16"), ("idn", 128, "bfloat16"), ("zer", 128, "bfloat16"),
+        ("kc", 1536, "bfloat16"), ("kj", 1024, "bfloat16"), ("eb", 2048, "bfloat16"), ("idn", 128, "bfloat16"), ("zer", 128, "bfloat16"),
         ("ione", 384, "int32"), ("itwo", 384, "int32"), ("mask", 384, "float32"), ("mmin", 384, "float32"), ("dzr", 384, "float32"), ("dzs", 384, "float32"), ("ramp", 384, "float32"),
-        ("jrow", 384, "float32"), ("jrev", 384, "float32"), ("kval", 192, "float32"), ("iok", 192, "bfloat16"), ("mske", 384, "float32"),
+        ("jrow", 384, "float32"), ("kval", 192, "float32"), ("iok", 192, "bfloat16"), ("mske", 384, "float32"),
         ("dst", 384, "float32"), ("sc", 384, "float32"), ("junk", 6624, "bfloat16"), ("ds", 384, "float32"), ("cm", 384, "float32"), ("cw", 384, "float32"), ("cb", 5632, "bfloat16"),
         ("hl", 96, "bfloat16"), ("exa", 768, "bfloat16"), ("ow", 384, "float32"), ("nx", 192, "float32"),
-        ("zd", 192, "bfloat16"), ("exb", 1536, "bfloat16"), ("kr", 384, "float32"), ("oht", 768, "bfloat16"), ("crm", 192, "float32"), ("crw", 192, "float32"),
+        ("krow", 384, "float32"), ("kr", 384, "float32"), ("oht", 768, "bfloat16"), ("crm", 192, "float32"), ("crw", 192, "float32"),
         ("lr", 384, "float32"), ("lm", 192, "float32"), ("sl", 192, "float32"), ("zt", 768, "bfloat16"),
         ("lrr", 192, "bfloat16"), ("dj", 1056, "bfloat16"), ("dg", 192, "float32"), ("dd", 192, "float32"), ("kvm", 192, "float32"),
         ("nw", 584, "float32"), ("ns", 384, "float32"), ("lmy", 384, "float32"), ("sly", 384, "float32"), ("yo", 384, "float32"), ("olt", 384, "float32"),
@@ -27,11 +27,11 @@ for _n, _w, _d in [
     SCRATCH[_n] = ("sbuf", [128, _w], _d)
     PLACE[_n] = (_n, 0, _w)
 for _b, _d, _l in [
-        ("cpk", "float32", [("pmf", 2), ("phf", 2), ("phx", 2), ("phy", 2), ("cqi", 24), ("cq", 24), ("kti", 12), ("ktp", 12), ("hfi", 4), ("jfi", 4), ("jf", 4), ("jh4", 4), ("jl4", 4),
+        ("cpk", "float32", [("pmf", 2), ("phf", 2), ("phx", 2), ("phy", 2), ("cqi", 24), ("cq", 24), ("cqf", 24), ("kti", 12), ("ktp", 12), ("hfi", 4), ("jfi", 4), ("jf", 4), ("jh4", 4), ("jl4", 4),
                             ("ufi", 8), ("gmi", 8), ("gm", 8)]),
         ("ipk", "int32", [("pint", 2), ("pmi", 2), ("phi", 2)]),
-        ("fpk", "float32", [("rs", 24), ("rq", 24), ("rq2", 24), ("qw", 24), ("vh", 96), ("mn", 96), ("mx", 96), ("sa", 48), ("sb", 48), ("um", 144), ("aw", 24), ("bw", 24), ("sp", 24), ("kwa", 24),
-                            ("kw", 24), ("fw", 24), ("dw", 24), ("fd", 24), ("mw", 24), ("zc", 48), ("kg", 48), ("ra", 4), ("rr", 4), ("sls", 12), ("du", 12), ("tot", 12), ("df", 12),
+        ("fpk", "float32", [("rs", 24), ("rq", 24), ("rq2", 24), ("qw", 24), ("vh", 96), ("mn", 96), ("mx", 96), ("sa", 48), ("sb", 48), ("um", 144), ("aw", 24), ("bw", 24), ("sp", 24),
+                            ("kw", 24), ("fw", 24), ("dw", 24), ("fd", 24), ("mw", 24), ("kg", 48), ("ra", 4), ("rr", 4), ("sls", 12), ("du", 12), ("tot", 12), ("df", 12),
                             ("dy", 12), ("dz", 12)]),
         ("uck", "uint16", [("u8", 8), ("hl48", 4)]),
         ("upk", "uint16", [("qo", 24), ("mo", 24), ("cof", 12), ("lo", 12), ("off", 12), ("no", 24), ("lyo", 24)])]:
@@ -54,7 +54,7 @@ def _codes(name, n):
 for _i in range(3):
     _codes("z%d" % _i, M)
     _codes("a%d" % _i, M)
-for _n, _w in [("x", C), ("u", 128), ("ur", 128), ("v", 128), ("k", 512), ("j", 256), ("e", 512), ("w", 512), ("c", 1408), ("b", 192), ("p", C), ("o", 192)]:
+for _n, _w in [("x", C), ("u", 128), ("ur", 128), ("v", 128), ("k", 384), ("j", 256), ("e", 512), ("w", 512), ("c", 1408), ("b", 192), ("o", 192)]:
     _codes("m" + _n, _w)
 SEMAPHORES = ["sv", "ss", "sp", "sg", "sent", "arr0", "arr1", "arr2"] + ["d%d" % i for i in range(24)]
 
@@ -158,8 +158,8 @@ def rank_program(g, core, T, topo):
     def W16(name, n):
         return V(name, 15, n, 16)
 
-    def ap(r):
-        return T[r[0]][:, r[1]:r[2]] if r[3] == 1 else T[r[0]][:, r[1]:r[2]:r[3]]
+    def ap(r, parts=128):
+        return T[r[0]][0:parts, r[1]:r[2]] if r[3] == 1 else T[r[0]][0:parts, r[1]:r[2]:r[3]]
 
     def src(r, off):
         return ap(r) if off is None else ap(r).indirect(ap(off))
@@ -220,14 +220,6 @@ def rank_program(g, core, T, topo):
     def select(out, a, pattern, op, fill, base, cm):
         call("g", [a], [out], lambda e: e.affine_select(ap(out), ap(a), pattern, op, fill, base, cm))
 
-    def expand(out, w, a, dv):
-        for h in range(7, -1, -1):
-            o = V(out, w * h, w * h + w)
-            if h < dv:
-                ts(o, V(a), V("gm", h, h + 1), A.mult)
-            else:
-                act(o, V(a), scale=V("gm", h, h + 1))
-
     def half(b):
         tt(V("w%d" % b, 0, C), V("t%d" % b), V("xs", b, 4 * C, 4), A.add, off=V("lyo"))
 
@@ -262,7 +254,6 @@ def rank_program(g, core, T, topo):
     for i, (n, cs) in enumerate(TILES):
         ms(V("cb", 4 * COFS[i] + 64 * cs[-1], 4 * (COFS[i] + n)), 0.0)
     ms(V("kc", 1024, 1536), 0.0)
-    ms(V("kc", 1536, 2048), 512.0)
     select(V("kc", 512, 1024), V("kc", 512, 1024), [[-16, 8], [0, 64]], A.is_ge, 0.0, 0, 1)
     select(V("kc", 512, 1024), V("kc", 512, 1024), [[16, 8], [0, 64]], A.is_ge, 0.0, 15, -1)
     select(V("idn"), V("idn"), [[-1, 128]], A.is_equal, 0.0, 0, 1)
@@ -270,8 +261,8 @@ def rank_program(g, core, T, topo):
     iota(V("cqi"), [[-16, 24]], 383, 0)
     iota(V("gmi"), [[1, 8]], 0, 0)
     iota(V("jrow"), [[1, 384]], 1, 0)
+    iota(V("mske"), [[1, 384]], 0, 0)
     iota(V("hfi"), [[1, 4]], 0, 0)
-    iota(V("jrev"), [[-1, 384]], 383, 0)
     iota(V("jfi"), [[16, 4]], 0, 1)
     iota(V("iok"), [[-1, 192]], 191, 0)
     iota(V("kti"), [[16, 12]], 385, 0)
@@ -288,8 +279,8 @@ def rank_program(g, core, T, topo):
         ms(V("zer"), 0.0)
         ms(V("hl"), 0.0)
         ms(V("du"), 0.0)
-        ms(V("zd"), 0.0)
         ts(V("cq"), V("cqi"), V("pmf", 0, 1), A.subtract)
+        ts(V("cqf"), V("cq"), 2.0 ** -9, A.mult)
         ts(V("gm"), V("gmi"), V("phf", 0, 1), A.is_equal)
         ts(V("phx"), V("phf"), 3.0, A.mult)
         ts(V("hl48"), V("hfi"), V("phx", 0, 1), A.add)
@@ -298,7 +289,6 @@ def rank_program(g, core, T, topo):
         ts(V("jh4"), V("jf"), RND, A.add, RND, A.subtract)
         tt(V("jl4"), V("jf"), V("jh4"), A.subtract)
         ts(V("ktp"), V("kti"), V("pmf", 0, 1), A.add)
-        ts(V("mske"), V("jrow"), 1.0, A.subtract)
         tt(V("mske"), V("mske"), V("mask"), A.mult)
 
     for t in range(R):
@@ -327,7 +317,7 @@ def rank_program(g, core, T, topo):
                 k = PACKS[i]
                 quant("mc", COFS[k], COFS[i] + n - COFS[k], "cb", 4 * COFS[k])
                 if t == 0 and i == 0:
-                    quant("mk", 0, 512, "kc")
+                    quant("mk", 0, 384, "kc")
                 for k in range(k, i + 1):
                     mm("ps5", TILES[k][0], "mk", 0 if k == 0 else 128, "mc", COFS[k], k == 0, k == 5)
             if t == 0 and i == 1:
@@ -343,17 +333,21 @@ def rank_program(g, core, T, topo):
         tt(V("qw"), V("rq2"), W16("cw", C), A.add)
         ts(V("hl", 0, 96, 4), V("qw"), RND, A.add, RND, A.subtract)
         tt(V("hl", 1, 96, 4), V("qw"), V("hl", 0, 96, 4), A.subtract)
-        expand("exa", 96, "hl", DA)
+        for h in range(7, -1, -1):
+            o = V("exa", 96 * h, 96 * h + 96)
+            if h < DA:
+                ts(o, V("hl"), V("gm", h, h + 1), A.mult)
+            else:
+                act(o, V("hl"), scale=V("gm", h, h + 1))
         quant("mb", 0, 192, "exa")
         mm("ps6", 192, "mk", 256, "mb", 0)
-        cp(V("qo"), V("qw"))
-        cp(V("ow"), V("jrow"), ooff=V("qo"))
         for b in range(4):
             act(V("t%d" % b), V("ps%d" % (1 + b), 0, C))
         act(V("nw", 1, C + 1), V("mske"))
         if t == 0:
             for k in range(4):
                 act(V("kj", k, 512, 4), V("zer"), F.Identity, bias=V("jh4", k, k + 1))
+                act(V("kj", 512 + k, 1024, 4), V("zer"), F.Identity, bias=V("jl4", k, k + 1))
         cp(V("vh"), V("ps6", 96, 192))
         tt(V("nx", 0, 192, 2), V("ps6", 0, 96), V("vh"), A.min)
         tt(V("nx", 1, 192, 2), V("ps6", 0, 96), V("vh"), A.max)
@@ -362,13 +356,12 @@ def rank_program(g, core, T, topo):
         tt(V("um", 0, 24), V("mn", 0, 48, 2), V("mn", 48, 96, 2), A.min)
         tt(V("um", 24, 48), V("mx", 1, 48, 2), V("mx", 49, 96, 2), A.max)
         tt(V("sp"), V("um", 24, 48), V("um", 0, 24), A.subtract)
-        tt(V("zc"), V("sp"), V("mask", 0, 48), A.mult, off=V("hl48", 0, 3))
-        ts(V("zd", 0, 192, 4), V("zc"), RND, A.add, RND, A.subtract)
-        ts(V("kwa"), V("sp"), 512.0, A.mult)
-        tt(V("zd", 1, 192, 4), V("zc"), V("zd", 0, 192, 4), A.subtract)
-        tt(V("kw"), V("kwa"), V("cq"), A.add)
-        expand("exb", 192, "zd", DB)
+        tt(V("kw"), V("sp"), V("cqf"), A.add)
+        dma("y", [V("kw")], [V("krow")], T.krow[0:1, :], ap(V("kw"), 16))
+        call("g", [V("krow")], [V("kr")], lambda e: e.partition_broadcast(T.kr[:], T.krow[0:1, :], 128))
         cp(V("kg"), V("kw"), off=V("hl48", 0, 3))
+        cp(V("qo"), V("qw"))
+        cp(V("ow"), V("jrow"), ooff=V("qo"))
         tt(V("sa"), V("mx", 0, 96, 2), V("mn", 1, 96, 2), A.min)
         tt(V("sb"), V("mx", 0, 96, 2), V("mn", 1, 96, 2), A.max)
         tt(V("um", 48, 72), V("mn", 0, 48, 2), V("mn", 48, 96, 2), A.max)
@@ -377,15 +370,12 @@ def rank_program(g, core, T, topo):
         tt(V("um", 120, 144), V("sa", 0, 24), V("sa", 24, 48), A.max)
         tt(V("aw"), V("um", 48, 72), V("um", 96, 120), A.max)
         tt(V("bw"), V("um", 72, 96), V("um", 120, 144), A.min)
-        quant("mp", 0, C, "exb")
-        mm("ps7", C, "mk", 384, "mp", 0)
         tt(V("um", 0, 24), V("aw"), V("bw"), A.min)
         tt(V("um", 24, 48), V("aw"), V("bw"), A.max)
         tt(V("fw"), V("qw"), V("um", 0, 24), A.is_le)
         tt(V("dw"), V("um", 24, 48), V("um", 0, 24), A.subtract)
         tt(V("fd"), V("fw"), V("dw"), A.mult)
         tt(V("mw"), V("fd"), V("um", 0, 24), A.add)
-        tt(V("kr"), V("ps7", 0, C), V("jrev"), A.add)
         for h in range(3):
             act(V("junk", 5472 + 384 * h, 5856 + 384 * h), V("kr"), F.Sign, scale=-1.0, bias=V("kg", 16 * h, 16 * h + 1), accum=V("ra", h, h + 1))
         act(V("rr", 0, 3), V("ra", 0, 3), F.Identity, scale=-0.5, bias=191.5)
@@ -394,17 +384,14 @@ def rank_program(g, core, T, topo):
         tt(V("lmy"), V("ow"), V("mask"), A.mult, off=V("mo"))
         scan(V("sly"), V("dzr"), V("lmy"), A.mult, A.add)
         ts(V("lyo"), W16("sly", C), -1.0, A.add)
-        half(0)
         if t == 0:
-            for k in range(4):
-                ts(V("kj", 512 + k, 1024, 4), V("zer"), V("jl4", k, k + 1), A.add)
             quant("mj", 0, 256, "kj")
         for h in range(3):
             ts(V("oht", h, 768, 4), V("iok"), V("rr", h, h + 1), A.is_equal)
         quant("mo", 0, 192, "oht")
         mm("ps6", 192, "mj", 0, "mo", 0, True, False)
         mm("ps6", 192, "mj", 128, "mo", 0, False, True)
-        half(1)
+        half(0)
         tt(V("crm"), V("ps6", 0, M), V("mask", 0, M), A.mult)
         scan(V("crw"), V("dzr", 0, M), V("crm"), A.mult, A.add)
         cp(V("cof"), W16("crw", M))
@@ -417,7 +404,6 @@ def rank_program(g, core, T, topo):
             cp(V("zt", b, 768, 4), V("t%d" % b), off=V("lo"))
         z, a = "z%d" % t, "a%d" % t
         ts(V("sls"), W16("sl", M), -192.0, A.add)
-        tt(V("kvm"), V("mask"), V("kval"), A.mult, off=V("lo"))
         quant(z, 0, M, "zt")
         dst = T.cores[(rank + 1 + t) % N]
         rid, pid = topo.addr(dst)[:2]
@@ -435,10 +421,11 @@ def rank_program(g, core, T, topo):
             else:
                 sumup(V("du", c, c + 1), V("dj", d, d + n))
             d += n
+        tt(V("kvm"), V("mask"), V("kval"), A.mult, off=V("lo"))
         tt(V("dg"), V("lr"), V("sl"), A.is_equal, off=V("cof"))
         scan(V("dd"), V("dzr", 0, M), V("dg"), A.mult, A.add)
-        half(2)
-        half(3)
+        for b in range(1, 4):
+            half(b)
         tt(V("tot"), V("du"), W16("dd", M), A.add)
         ts(V("df"), V("tot"), 1.0, A.subtract, 1.0, A.min)
         tt(V("dy"), V("df"), V("ktp"), A.mult)

from concourse.mybir import dt, AluOpType as A, AxisListType, ActivationFunctionType as F

C, M, R, N = 384, 192, 3, 8
DA = 6
DR, DE = 2, 9
DG = 3
BIG = 1.0e29
RND = 402653184.0
TILES = [(384, [23, 22, 21]), (320, [20, 19, 18, 17]), (256, [16, 15, 14, 13]), (192, [12, 11, 10, 9]), (128, [8, 7, 6, 5]), (128, [4, 3, 2, 1])]
COFS = [0, 384, 704, 960, 1152, 1280]
PACKS = {0: 0, 1: 1, 3: 2, 5: 4}

SCRATCH, PLACE = {}, {}
for _n, _w, _d in [
        ("xs", 1536, "bfloat16"), ("ub", 512, "bfloat16"), ("vb", 512, "bfloat16"),
        ("kc", 1536, "bfloat16"), ("kj", 1024, "bfloat16"), ("eb", 2048, "bfloat16"), ("idn", 128, "bfloat16"), ("zer", 128, "bfloat16"),
        ("ione", 384, "int32"), ("itwo", 384, "int32"), ("mask", 384, "float32"), ("mmin", 384, "float32"), ("dzr", 384, "float32"), ("dzs", 384, "float32"), ("ramp", 384, "float32"),
        ("jrow", 384, "float32"), ("kval", 192, "float32"), ("iok", 192, "bfloat16"), ("mske", 384, "float32"),
        ("dst", 384, "float32"), ("sc", 384, "float32"), ("junk", 6624, "bfloat16"), ("ds", 384, "float32"), ("cm", 384, "float32"), ("cw", 384, "float32"), ("cb", 5632, "bfloat16"),
        ("hl", 96, "bfloat16"), ("exa", 768, "bfloat16"), ("ow", 384, "float32"), ("nx", 192, "float32"),
        ("krow", 384, "float32"), ("kr", 384, "float32"), ("oht", 768, "bfloat16"), ("crm", 192, "float32"), ("crw", 192, "float32"),
        ("lr", 384, "float32"), ("lm", 192, "float32"), ("sl", 192, "float32"), ("zt", 768, "bfloat16"),
        ("lrr", 192, "bfloat16"), ("dj", 1056, "bfloat16"), ("dg", 192, "float32"), ("dd", 192, "float32"), ("kvm", 192, "float32"),
        ("nw", 584, "float32"), ("ns", 384, "float32"), ("lmy", 384, "float32"), ("sly", 384, "float32"), ("yo", 384, "float32"), ("olt", 384, "float32"),
        ("t0", 384, "bfloat16"), ("t1", 384, "bfloat16"), ("t2", 384, "bfloat16"), ("t3", 384, "bfloat16"),
        ("w0", 576, "float32"), ("w1", 576, "float32"), ("w2", 576, "float32"), ("w3", 576, "float32")]:
    SCRATCH[_n] = ("sbuf", [128, _w], _d)
    PLACE[_n] = (_n, 0, _w)
for _b, _d, _l in [
        ("cpk", "float32", [("pmf", 2), ("phf", 2), ("phx", 2), ("phy", 2), ("cqi", 24), ("cq", 24), ("cqf", 24), ("kti", 12), ("ktp", 12), ("hfi", 4), ("jfi", 4), ("jf", 4), ("jh4", 4), ("jl4", 4),
                            ("ufi", 8), ("gmi", 8), ("gm", 8)]),
        ("ipk", "int32", [("pint", 2), ("pmi", 2), ("phi", 2)]),
        ("fpk", "float32", [("rs", 24), ("rq", 24), ("rq2", 24), ("qw", 24), ("vh", 96), ("mn", 96), ("mx", 96), ("sa", 48), ("sb", 48), ("um", 144), ("aw", 24), ("bw", 24), ("sp", 24),
                            ("kw", 24), ("fw", 24), ("dw", 24), ("fd", 24), ("mw", 24), ("kg", 48), ("ra", 4), ("rr", 4), ("sls", 12), ("du", 12), ("tot", 12), ("df", 12),
                            ("dy", 12), ("dz", 12)]),
        ("uck", "uint16", [("u8", 8), ("hl48", 4)]),
        ("upk", "uint16", [("qo", 24), ("mo", 24), ("cof", 12), ("lo", 12), ("off", 12), ("no", 24), ("lyo", 24)])]:
    _o = 0
    for _n, _w in _l:
        PLACE[_n] = (_b, _o, _w)
        _o += (_w + 7) // 8 * 8
    SCRATCH[_b] = ("sbuf", [128, _o], _d)
for _i in range(8):
    SCRATCH["ps%d" % _i] = ("psum", [128, 512], "float32")
    PLACE["ps%d" % _i] = ("ps%d" % _i, 0, 512)


def _codes(name, n):
    for k, d in (("q", "float8_e4m3fn_x4"), ("s", "uint8")):
        SCRATCH[name + k] = ("sbuf", [128, n], d)
        PLACE[name + k] = (name + k, 0, n)


for _i in range(3):
    _codes("z%d" % _i, M)
    _codes("a%d" % _i, M)
for _n, _w in [("x", C), ("u", 128), ("ur", 128), ("v", 128), ("k", 384), ("j", 256), ("e", 512), ("w", 512), ("c", 1408), ("b", 192), ("o", 192)]:
    _codes("m" + _n, _w)
SEMAPHORES = ["sv", "ss", "sp", "sg", "sent", "arr0", "arr1", "arr2"] + ["d%d" % i for i in range(24)]


def builder(g, T):
    eng = {"v": g.vector, "s": g.scalar, "p": g.tensor, "g": g, "y": g.sync}
    cnt = {"v": 0, "s": 0, "p": 0, "g": 0}
    know = {e: {} for e in eng}
    acc, ndma = {}, [0]

    def reg(r):
        return (r[0], 0, 512, 1) if r[0][:2] == "ps" else r

    def meet(a, b):
        if a[1] >= b[2] or b[1] >= a[2]:
            return False
        return not (a[3] == b[3] and a[3] > 1 and (a[1] - b[1]) % a[3])

    def sync(e, reads, writes, extra=()):
        want = {}
        k = know[e]

        def need(sem, n, snap):
            if k.get(sem, 0) < n and want.get(sem, (0, None))[0] < n:
                want[sem] = (n, snap)
        for kind, rs in (("r", reads), ("w", writes)):
            for r in rs:
                r = reg(r)
                ps = r[0][:2] == "ps"
                for (k2, r2, e2, sem, n, snap) in acc.get(r[0], []):
                    if not meet(r, r2):
                        continue
                    if kind == "r" and k2 == "r" and not (ps and e != e2):
                        continue
                    if e == e2 and sem[0] == "s" and k2 == "r":
                        continue
                    if e == e2 == "p" and ps:
                        continue
                    need(sem, n, snap)
        for sem, n in extra:
            need(sem, n, {})
        for sem in sorted(want, key=lambda s: -len(want[s][1])):
            n, snap = want[sem]
            if k.get(sem, 0) >= n:
                continue
            eng[e].wait_ge(T.sem[sem], n)
            k[sem] = n
            for s2 in snap:
                if k.get(s2, 0) < snap[s2]:
                    k[s2] = snap[s2]

    def note(e, reads, writes, sem, n):
        snap = dict(know[e])
        for r in writes:
            r = reg(r)
            old = acc.get(r[0], [])
            if r[3] == 1:
                old = [o for o in old if not (o[1][1] >= r[1] and o[1][2] <= r[2])]
            acc[r[0]] = old + [("w", r, e, sem, n, snap)]
        for r in reads:
            r = reg(r)
            old = [o for o in acc.get(r[0], []) if not (o[0] == "r" and o[2] == e and o[3] == sem and o[1] == r)]
            acc[r[0]] = old + [("r", r, e, sem, n, snap)]

    def call(e, reads, writes, make, extra=()):
        sync(e, reads, writes, extra)
        cnt[e] += 1
        make(eng[e]).then_inc(T.sem["s" + e], 1)
        note(e, reads, writes, "s" + e, cnt[e])

    def dma(e, reads, writes, out, in_):
        sync(e, reads, writes)
        sem = "d%d" % ndma[0]
        ndma[0] += 1
        eng[e].dma_start(out, in_).then_inc(T.sem[sem], 16)
        note(e, reads, writes, sem, 16)

    def send(reads, make):
        sync("g", reads, [])
        make()

    def finish():
        for e in ("v", "s", "p", "g"):
            if cnt[e] and know["g"].get("s" + e, 0) < cnt[e]:
                g.wait_ge(T.sem["s" + e], cnt[e])
        for i in range(ndma[0]):
            g.wait_ge(T.sem["d%d" % i], 16)
    return call, dma, send, finish


def rank_program(g, core, T, topo):
    rank = T.rank_of(core)
    if rank is None:
        return
    call, dma, send, finish = builder(g, T)

    def V(name, lo=0, hi=None, st=1):
        b, o, w = PLACE[name]
        return (b, o + lo, o + (w if hi is None else hi), st)

    def W16(name, n):
        return V(name, 15, n, 16)

    def ap(r, parts=128):
        return T[r[0]][0:parts, r[1]:r[2]] if r[3] == 1 else T[r[0]][0:parts, r[1]:r[2]:r[3]]

    def src(r, off):
        return ap(r) if off is None else ap(r).indirect(ap(off))

    def rd(*rs):
        return [r for r in rs if isinstance(r, tuple)]

    def val(s):
        return ap(s) if isinstance(s, tuple) else s

    def tt(out, a, b, op, off=None):
        call("v", rd(a, b, off), [out], lambda e: e.tensor_tensor(ap(out), src(a, off), ap(b), op))

    def ts(out, a, s1, op0, s2=None, op1=None, off=None):
        if op1 is None:
            call("v", rd(a, s1, off), [out], lambda e: e.tensor_scalar(ap(out), src(a, off), val(s1), None, op0))
        else:
            call("v", rd(a, s1, s2, off), [out], lambda e: e.tensor_scalar(ap(out), src(a, off), val(s1), val(s2), op0, op1))

    def cp(out, a, off=None, ooff=None):
        call("v", rd(a, off, ooff), [out], lambda e: e.tensor_copy(src(out, ooff), src(a, off)))

    def ms(out, c):
        call("v", [], [out], lambda e: e.memset(ap(out), c))

    def sumup(out, a):
        call("v", [a], [out], lambda e: e.tensor_reduce(ap(out), ap(a), AxisListType.X, A.add))

    def scan(out, d0, d1, op0, op1):
        call("v", [d0, d1], [out], lambda e: e.tensor_tensor_scan(ap(out), ap(d0), ap(d1), 0.0, op0, op1))

    def act(out, a, func=F.Copy, scale=1.0, bias=0.0, accum=None, off=None):
        kw = {}
        if isinstance(scale, tuple) or scale != 1.0:
            kw["scale"] = val(scale)
        if isinstance(bias, tuple) or bias != 0.0:
            kw["bias"] = val(bias)
        if accum is not None:
            kw["accum_out"] = ap(accum)
        call("s", rd(a, scale, bias, off), [out] + rd(accum), lambda e: e.activation(ap(out), src(a, off), func, **kw))

    def quant(q, lo, n, tile, tlo=0):
        o, s, i = V(q + "q", lo, lo + n), V(q + "s", lo, lo + n), V(tile, tlo, tlo + 4 * n)
        call("v", [i], [o, s], lambda e: e.quantize_mx(ap(o), ap(s), ap(i)))

    def mm(ps, n, l, llo, r, rlo, start=True, stop=True, extra=()):
        lc, lsc = V(l + "q", llo, llo + 128), V(l + "s", llo, llo + 128)
        rc, rsc = V(r + "q", rlo, rlo + n), V(r + "s", rlo, rlo + n)
        o = (ps, 0, n, 1)
        call("p", [lc, lsc, rc, rsc], [o], lambda e: e.matmul_mx(ap(o), ap(lc), ap(lsc), ap(rc), ap(rsc), start, stop), extra)

    def iota(out, pattern, base, cm):
        if SCRATCH[out[0]][2] == "int32":
            call("g", [], [out], lambda e: e.iota(ap(out), pattern, base, cm))
        else:
            call("g", [], [out], lambda e: e.iota(ap(out), pattern, base, cm, allow_small_or_imprecise_dtypes=True))

    def select(out, a, pattern, op, fill, base, cm):
        call("g", [a], [out], lambda e: e.affine_select(ap(out), ap(a), pattern, op, fill, base, cm))

    def half(b):
        tt(V("w%d" % b, 0, C), V("t%d" % b), V("xs", b, 4 * C, 4), A.add, off=V("lyo"))

    dma("y", [], [V("ub")], T.ub[:], T.u[:])
    dma("s", [], [V("xs")], T.xs[:], T.x[:])
    dma("y", [], [V("mwq")], T.mwq[:].bitcast(dt.uint8), T.wc[:])
    dma("y", [], [V("mws")], T.mws[:], T.ws[:])
    dma("y", [], [V("vb")], T.vb[:], T.v[:])

    iota(V("ufi"), [[16, 8]], 0, 0)
    iota(V("pint"), [[0, 2]], 0, 1)
    iota(V("ione"), [[1, 384]], 128, -1)
    iota(V("ramp"), [[0, 24], [1, 16]], 0, 0)
    cp(V("u8"), V("ufi"))
    ms(V("kc", 512, 1024), -1.0)
    ms(V("idn"), 1.0)
    ms(V("rs"), 0.0)
    ts(V("phi"), V("pint"), 4, A.arith_shift_right)
    ts(V("pmi"), V("pint"), 15, A.bitwise_and)
    cp(V("phf"), V("phi"))
    cp(V("pmf"), V("pmi"))
    ts(V("itwo"), V("ione"), 15, A.bitwise_and)
    ts(V("mask"), V("itwo"), 0, A.is_equal)
    ts(V("dzr"), V("ramp"), 1.0, A.min)
    act(V("mmin"), V("mask"), F.Identity, scale=2 * BIG, bias=-BIG)
    act(V("dzs"), V("dzr"), F.Identity, scale=2 * BIG, bias=-BIG)
    quant("mu", 0, 128, "ub")
    o8 = V("u8")
    call("v", [V("muq"), o8], [V("murq")], lambda e: e.tensor_copy(T.murq[:].bitcast(dt.uint32), T.muq[:].bitcast(dt.uint32).indirect(ap(o8))))
    call("s", [V("mus"), o8], [V("murs")], lambda e: e.activation(T.murs[:], T.mus[:].indirect(ap(o8)), F.Copy))
    quant("mx", 0, C, "xs")
    for i, (n, cs) in enumerate(TILES):
        ms(V("cb", 4 * COFS[i] + 64 * cs[-1], 4 * (COFS[i] + n)), 0.0)
    ms(V("kc", 1024, 1536), 0.0)
    select(V("kc", 512, 1024), V("kc", 512, 1024), [[-16, 8], [0, 64]], A.is_ge, 0.0, 0, 1)
    select(V("kc", 512, 1024), V("kc", 512, 1024), [[16, 8], [0, 64]], A.is_ge, 0.0, 15, -1)
    select(V("idn"), V("idn"), [[-1, 128]], A.is_equal, 0.0, 0, 1)
    iota(V("eb"), [[0, 2048]], 0, 0)
    iota(V("cqi"), [[-16, 24]], 383, 0)
    iota(V("gmi"), [[1, 8]], 0, 0)
    iota(V("jrow"), [[1, 384]], 1, 0)
    iota(V("mske"), [[1, 384]], 0, 0)
    iota(V("hfi"), [[1, 4]], 0, 0)
    iota(V("jfi"), [[16, 4]], 0, 1)
    iota(V("iok"), [[-1, 192]], 191, 0)
    iota(V("kti"), [[16, 12]], 385, 0)
    iota(V("kval"), [[1, 192]], 384, 0)
    iota(V("oht"), [[0, 768]], 0, 0)
    act(V("kc", 1024, 1536, 4), V("mask", 0, 128))
    act(V("kc", 1025, 1536, 4), V("mask", 0, 128))
    act(V("kc", 0, 512), V("kc", 512, 1024))
    act(V("kc", 3, 512, 4), V("kc", 515, 1024, 4), scale=-1.0)

    def late_constants():
        for b in range(4):
            act(V("eb", 512 * b + b, 512 * b + 512, 4), V("idn"))
        ms(V("zer"), 0.0)
        ms(V("hl"), 0.0)
        ms(V("du"), 0.0)
        ts(V("cq"), V("cqi"), V("pmf", 0, 1), A.subtract)
        ts(V("cqf"), V("cq"), 2.0 ** -9, A.mult)
        ts(V("gm"), V("gmi"), V("phf", 0, 1), A.is_equal)
        ts(V("phx"), V("phf"), 3.0, A.mult)
        ts(V("hl48"), V("hfi"), V("phx", 0, 1), A.add)
        ts(V("phy"), V("phf"), 32.0, A.mult)
        ts(V("jf"), V("jfi"), V("phy", 0, 1), A.add)
        ts(V("jh4"), V("jf"), RND, A.add, RND, A.subtract)
        tt(V("jl4"), V("jf"), V("jh4"), A.subtract)
        ts(V("ktp"), V("kti"), V("pmf", 0, 1), A.add)
        tt(V("mske"), V("mske"), V("mask"), A.mult)

    for t in range(R):
        if t:
            quant("mx", 0, C, "xs")
        mm("ps0", C, "mur", 0, "mx", 0)
        tt(V("dst"), V("ps0", 0, C), V("mmin"), A.min)
        scan(V("sc"), V("dzs"), V("dst"), A.min, A.max)
        jk = 0
        for i, (n, cs) in enumerate(TILES):
            o = 4 * COFS[i]
            if i == (4 if t == 0 else 0):
                if t == 0:
                    quant("me", 0, 512, "eb")
                for b in range(4):
                    mm("ps%d" % (1 + b), C, "me", 128 * b, "mx", 0)
            for w, c in enumerate(cs):
                ts(V("cb", o + w, o + 64 * c, 4), V("ps0", 0, 16 * c), V("sc", 16 * c + 15, 16 * c + 16), A.is_ge)
            if i == 0:
                tt(V("cb", 3, 4 * C, 4), V("ps0", 0, C), V("sc"), A.is_le)
            for w, c in enumerate(cs):
                if c > DR:
                    act(V("junk", jk, jk + 16 * c), V("cb", o + w, o + 64 * c, 4), accum=V("rs", c, c + 1))
                    jk += 16 * c
            if i in PACKS:
                k = PACKS[i]
                quant("mc", COFS[k], COFS[i] + n - COFS[k], "cb", 4 * COFS[k])
                if t == 0 and i == 0:
                    quant("mk", 0, 384, "kc")
                for k in range(k, i + 1):
                    mm("ps5", TILES[k][0], "mk", 0 if k == 0 else 128, "mc", COFS[k], k == 0, k == 5)
            if t == 0 and i == 1:
                late_constants()
        for w, c in enumerate(TILES[5][1]):
            if c <= DR:
                sumup(V("rs", c, c + 1), V("cb", 4 * COFS[5] + w, 4 * COFS[5] + 64 * c, 4))
        scan(V("ds"), V("dzr"), V("cb", 3, 4 * C, 4), A.mult, A.add)
        tt(V("rq"), V("cq"), W16("ds", C), A.subtract)
        tt(V("cm"), V("ps5", 0, C), V("mask"), A.mult)
        scan(V("cw"), V("dzr"), V("cm"), A.mult, A.add)
        tt(V("rq2"), V("rq"), V("rs"), A.add)
        tt(V("qw"), V("rq2"), W16("cw", C), A.add)
        ts(V("hl", 0, 96, 4), V("qw"), RND, A.add, RND, A.subtract)
        tt(V("hl", 1, 96, 4), V("qw"), V("hl", 0, 96, 4), A.subtract)
        for h in range(7, -1, -1):
            o = V("exa", 96 * h, 96 * h + 96)
            if h < DA:
                ts(o, V("hl"), V("gm", h, h + 1), A.mult)
            else:
                act(o, V("hl"), scale=V("gm", h, h + 1))
        quant("mb", 0, 192, "exa")
        mm("ps6", 192, "mk", 256, "mb", 0)
        for b in range(4):
            act(V("t%d" % b), V("ps%d" % (1 + b), 0, C))
        act(V("nw", 1, C + 1), V("mske"))
        if t == 0:
            for k in range(4):
                act(V("kj", k, 512, 4), V("zer"), F.Identity, bias=V("jh4", k, k + 1))
                act(V("kj", 512 + k, 1024, 4), V("zer"), F.Identity, bias=V("jl4", k, k + 1))
        cp(V("vh"), V("ps6", 96, 192))
        tt(V("nx", 0, 192, 2), V("ps6", 0, 96), V("vh"), A.min)
        tt(V("nx", 1, 192, 2), V("ps6", 0, 96), V("vh"), A.max)
        tt(V("mn"), V("nx", 0, 96), V("nx", 96, 192), A.min)
        tt(V("mx"), V("nx", 0, 96), V("nx", 96, 192), A.max)
        tt(V("um", 0, 24), V("mn", 0, 48, 2), V("mn", 48, 96, 2), A.min)
        tt(V("um", 24, 48), V("mx", 1, 48, 2), V("mx", 49, 96, 2), A.max)
        tt(V("sp"), V("um", 24, 48), V("um", 0, 24), A.subtract)
        tt(V("kw"), V("sp"), V("cqf"), A.add)
        dma("y", [V("kw")], [V("krow")], T.krow[0:1, :], ap(V("kw"), 16))
        call("g", [V("krow")], [V("kr")], lambda e: e.partition_broadcast(T.kr[:], T.krow[0:1, :], 128))
        cp(V("kg"), V("kw"), off=V("hl48", 0, 3))
        cp(V("qo"), V("qw"))
        cp(V("ow"), V("jrow"), ooff=V("qo"))
        tt(V("sa"), V("mx", 0, 96, 2), V("mn", 1, 96, 2), A.min)
        tt(V("sb"), V("mx", 0, 96, 2), V("mn", 1, 96, 2), A.max)
        tt(V("um", 48, 72), V("mn", 0, 48, 2), V("mn", 48, 96, 2), A.max)
        tt(V("um", 72, 96), V("mx", 1, 48, 2), V("mx", 49, 96, 2), A.min)
        tt(V("um", 96, 120), V("sb", 0, 24), V("sb", 24, 48), A.min)
        tt(V("um", 120, 144), V("sa", 0, 24), V("sa", 24, 48), A.max)
        tt(V("aw"), V("um", 48, 72), V("um", 96, 120), A.max)
        tt(V("bw"), V("um", 72, 96), V("um", 120, 144), A.min)
        tt(V("um", 0, 24), V("aw"), V("bw"), A.min)
        tt(V("um", 24, 48), V("aw"), V("bw"), A.max)
        tt(V("fw"), V("qw"), V("um", 0, 24), A.is_le)
        tt(V("dw"), V("um", 24, 48), V("um", 0, 24), A.subtract)
        tt(V("fd"), V("fw"), V("dw"), A.mult)
        tt(V("mw"), V("fd"), V("um", 0, 24), A.add)
        for h in range(3):
            act(V("junk", 5472 + 384 * h, 5856 + 384 * h), V("kr"), F.Sign, scale=-1.0, bias=V("kg", 16 * h, 16 * h + 1), accum=V("ra", h, h + 1))
        act(V("rr", 0, 3), V("ra", 0, 3), F.Identity, scale=-0.5, bias=191.5)
        cp(V("mo"), V("mw"))
        act(V("lr"), V("ow"), off=V("mo"))
        tt(V("lmy"), V("ow"), V("mask"), A.mult, off=V("mo"))
        scan(V("sly"), V("dzr"), V("lmy"), A.mult, A.add)
        ts(V("lyo"), W16("sly", C), -1.0, A.add)
        if t == 0:
            quant("mj", 0, 256, "kj")
        for h in range(3):
            ts(V("oht", h, 768, 4), V("iok"), V("rr", h, h + 1), A.is_equal)
        quant("mo", 0, 192, "oht")
        mm("ps6", 192, "mj", 0, "mo", 0, True, False)
        mm("ps6", 192, "mj", 128, "mo", 0, False, True)
        half(0)
        tt(V("crm"), V("ps6", 0, M), V("mask", 0, M), A.mult)
        scan(V("crw"), V("dzr", 0, M), V("crm"), A.mult, A.add)
        cp(V("cof"), W16("crw", M))
        tt(V("lm"), V("lr"), V("mask", 0, M), A.mult, off=V("cof"))
        scan(V("sl"), V("dzr", 0, M), V("lm"), A.mult, A.add)
        ts(V("lo"), W16("sl", M), -1.0, A.add)
        for b in (2, 3):
            act(V("zt", b, 768, 4), V("t%d" % b), off=V("lo"))
        for b in (0, 1):
            cp(V("zt", b, 768, 4), V("t%d" % b), off=V("lo"))
        z, a = "z%d" % t, "a%d" % t
        ts(V("sls"), W16("sl", M), -192.0, A.add)
        quant(z, 0, M, "zt")
        dst = T.cores[(rank + 1 + t) % N]
        rid, pid = topo.addr(dst)[:2]
        mask = topo.mask(core, dst)
        arr = T.sem["arr%d" % t]
        send([V(z + "q")], lambda: g.remote_dma(T[a + "q"][:].bitcast(dt.uint8), T[z + "q"][:].bitcast(dt.uint8), arr, T.sem.sent, pid, rid, mask))
        send([V(z + "s")], lambda: g.remote_dma(T[a + "s"][:], T[z + "s"][:], arr, T.sem.sent, pid, rid, mask))
        act(V("lrr"), V("lr"), F.Identity, bias=-192.0, off=V("cof"))
        d = 0
        for c in range(11):
            n = M - 16 * (c + 1)
            ts(V("dj", d, d + n), V("lrr", 16 * (c + 1), M), V("sls", c, c + 1), A.is_equal)
            if c < DE:
                act(V("junk", 4416 + d, 4416 + d + n), V("dj", d, d + n), accum=V("du", c, c + 1))
            else:
                sumup(V("du", c, c + 1), V("dj", d, d + n))
            d += n
        tt(V("kvm"), V("mask"), V("kval"), A.mult, off=V("lo"))
        tt(V("dg"), V("lr"), V("sl"), A.is_equal, off=V("cof"))
        scan(V("dd"), V("dzr", 0, M), V("dg"), A.mult, A.add)
        for b in range(1, 4):
            half(b)
        tt(V("tot"), V("du"), W16("dd", M), A.add)
        ts(V("df"), V("tot"), 1.0, A.subtract, 1.0, A.min)
        tt(V("dy"), V("df"), V("ktp"), A.mult)
        tt(V("dz"), V("dy"), W16("sl", M), A.max)
        cp(V("off"), V("dz"))
        cp(V("nw"), V("kvm"), ooff=V("off"))
        scan(V("ns"), V("dzr"), V("nw", 1, C + 1), A.mult, A.add)
        cp(V("no"), W16("ns", C))
        if t == R - 1:
            act(V("olt"), V("lr"), F.Identity, bias=-1.0)
            dma("y", [V("olt")], [], T.ol[:], T.olt[0:128:16, :])
            quant("mv", 0, 128, "vb")
        came = topo.engines(T.cores[(rank - 1 - t) % N], core)
        for b in range(4):
            mm("ps%d" % (1 + b), M, "mw", 128 * b, a, 0, extra=[("arr%d" % t, 2 * len(came))])
        for b in range(4):
            act(V("w%d" % b, C, C + M), V("ps%d" % (1 + b), 0, M), scale=0.0625)
        for b in range(4):
            o = V("xs", b, 4 * C, 4)
            if b < DG:
                ts(o, V("w%d" % b), 0.5, A.mult, off=V("no"))
            else:
                act(o, V("w%d" % b), scale=0.5, off=V("no"))
    quant("mx", 0, C, "xs")
    mm("ps0", C, "mv", 0, "mx", 0)
    dma("y", [V("mxq")], [], T.oc[:], T.mxq[:].bitcast(dt.uint8))
    for k in range(4):
        dma("y", [V("mxs")], [], T.osc[4 * k:4 * k + 4, :], T.mxs[32 * k:32 * k + 4, :])
    act(V("yo"), V("ps0", 0, C))
    dma("s", [V("yo")], [], T.y[:], T.yo[:])
    finish()
    g.wait_ge(T.sem.sent, sum(2 * len(topo.engines(core, T.cores[(rank + 1 + t) % N])) for t in range(R)))
